import numpy as np, ml_dtypes
CORES = [23,119,17,113]
N = 4
import mx_ref
BF = ml_dtypes.bfloat16
def cut(t, i, w=512):
    return t[:, w * i:w * i + w]
def tile(rs):
    return np.stack(rs, axis=2).reshape(128, -1).astype(BF)
def pick(q, e):
    c = np.concatenate([q[0].reshape(128, -1, 4), np.zeros((128, 1, 4), np.uint8)], axis=1); s = np.concatenate([q[1], np.ones((16, 1), np.uint8)], axis=1)
    return (np.ascontiguousarray(c[:, e].reshape(128, -1)), np.ascontiguousarray(s[:, e]))
def join(*qs):
    return (np.concatenate([q[0] for q in qs], axis=1), np.concatenate([q[1] for q in qs], axis=1))
def put(q, e, v):
    c, s = q[0].reshape(128, -1, 4).copy(), q[1].copy(); c[:, e] = v[0].reshape(128, -1, 4); s[:, e] = v[1]
    return (c.reshape(128, -1), s)
def pk(c, s):
    return (np.ascontiguousarray(c), mx_ref.live(s))
def emit(q):
    return q[0], q[1]
def f(rng, *shape):
    return mx_ref.flush((rng.standard_normal(shape, dtype=np.float32) * np.exp2(rng.integers(-2, 3, shape[:-1] + (1,)))).astype(BF))
def wide(rng, *shape, cols=0):
    v = rng.standard_normal(shape, dtype=np.float32) * np.exp2(rng.integers(-12, 13, shape)).astype(np.float32)
    if cols: v *= np.repeat(np.exp2(rng.integers(-cols, cols + 1, shape[:-2] + (1, shape[-1] // 4))) * (rng.random(shape[:-2] + (1, shape[-1] // 4)) > 0.0625), 4, axis=-1).astype(np.float32)
    return mx_ref.flush(v.astype(BF))
T, G, CS, R = 96, 128, 24, 4
def game(x, qx, w, u):
    wq = [[mx_ref.quantize(np.ascontiguousarray(cut(w[r], i))) for i in range(4)] for r in range(N)]
    uq = [mx_ref.quantize(np.ascontiguousarray(u[r])) for r in range(N)]
    wait = join(*[mx_ref.quantize(np.ascontiguousarray(qx[m])) for m in range(N)])
    s = [mx_ref.quantize(np.ascontiguousarray(x[r])) for r in range(N)]
    num = [r * T + np.arange(T) for r in range(N)]
    log, said, made, head = [[] for r in range(N)], [[] for r in range(N)], [], 0
    for t in range(R):
        for r in range(N):
            a = tile([np.maximum(mx_ref.matmul(wq[r][i], s[r]), np.float32(0)) * np.float32(0.0625) for i in range(4)])
            made.append(a)
            s[r] = mx_ref.quantize(a)
            h = mx_ref.matmul(uq[r], s[r])[:2] + np.float32(0)
            stop = np.flatnonzero(h[0] > h[1])[:CS]
            if stop.size == 0: continue
            log[r].append(pick(s[r], stop))
            said[r].extend(num[r][stop].tolist())
            g = head + np.arange(stop.size)
            s[r] = put(s[r], stop, pick(wait, G * (g % N) + g // N))
            num[r][stop] = N * T + g
            head += stop.size
    return log, said, s, num, made
def fit(d, top=2.0 ** 30):
    try:
        with np.errstate(all="ignore"):
            a = np.abs(np.stack(game(d["x"], d["qx"], d["w"], d["u"])[4]).astype(np.float32))
    except Exception: return False
    return bool(np.isfinite(a).all() and ((a == 0) | (a >= 2.0 ** -30) & (a <= top)).all())
def first(make, top=2.0 ** 30):
    for i in range(5):
        d = make()
        if fit(d, top): break
    return d
def plain(rng):
    w = np.rint(rng.standard_normal((N, 128, 2048), dtype=np.float32) * 8) * 0.125 * np.exp2(rng.integers(-1, 2, (N, 128, 1))) + 0.0
    u = np.zeros((N, 128, 512), np.float32)
    u[:, :, :8] = rng.standard_normal((N, 128, 8))
    u[:, :, 4:8] += 0.15 * rng.random((N, 1, 1))
    u *= np.exp2(rng.integers(-1, 2, (N, 128, 1)))
    return {"x": np.array(f(rng, N, 128, 4 * T)), "qx": np.array(f(rng, N, 128, 4 * G)), "w": w.astype(BF), "u": np.array(mx_ref.flush(u.astype(BF))), "v": np.array(f(rng, N, 128, 512))}
def channel(w, alone=False):
    a = w.astype(np.float32).reshape(N, 128, 4, 128, 4)
    if alone: a[:, :8] = 0
    a[:, :, :, :8, :] = 0
    for i in range(4):
        for j in range(8): a[:, j, i, j, i] = 16
    return a.reshape(N, 128, 2048).astype(BF)
def flags(d, live, wait):
    d["x"][:, :8] = np.repeat(np.where(live, 4.0, 0.0), 4, axis=1)[:, None, :].astype(BF)
    d["qx"][:, :8] = np.repeat(np.where(wait.reshape(G, N).T, 4.0, 0.0), 4, axis=1)[:, None, :].astype(BF)
def signed(t, a, b):
    o = np.abs(t.astype(np.float32))
    o[:, :4] *= a
    o[:, 4:8] *= b
    return o.astype(BF)
def setup_inputs(rng):
    return first(lambda: plain(rng), 2.0 ** 8)
def setup_inputs_many(rng):
    def make():
        d = plain(rng)
        d["w"] = channel(d["w"])
        pair = rng.integers(0, 2, N * G // 2)
        flags(d, np.stack([rng.permutation(T) < 3 * T // 4 for r in range(N)]), np.stack([pair, 1 - pair], axis=1).reshape(-1) == 1)
        for r in range(N):
            a = np.zeros((128, 512), np.float32)
            a[:8, :4] = 1
            a[8:, 4:8] = np.abs(rng.standard_normal((120, 4))) * 2.0 ** -8
            d["u"][r] = mx_ref.flush(a.astype(BF))
        return d
    return first(make)
def setup_inputs_none(rng):
    def make():
        d = plain(rng)
        a, b = rng.permutation(N)[:2]
        d["u"][a] = signed(d["u"][a], -1, 1)
        d["u"][b] = signed(d["u"][b], 1, -1)
        return d
    return first(make)
def setup_inputs_ties(rng):
    def make():
        d = plain(rng)
        d["w"] = channel(d["w"])
        flags(d, np.stack([rng.permutation(T) < T // 3 for r in range(N)]), rng.random(N * G) < 0.3)
        d["u"][:, :, 4:8] = d["u"][:, :, :4]
        d["u"][:, :8, :4] = 1
        d["u"][:, :8, 4:8] = 0
        a, c = rng.permutation(N)[:2]
        d["u"][a, :, 4:8] = d["u"][a, :, :4]
        d["u"][c] = 0
        d["u"][c, :7, :8] = 1
        d["u"][c, 7, :4] = 2.0 ** -8
        d["u"][c, 7, 4:8] = 2.0 ** -9
        return d
    return first(make)
def setup_inputs_zero(rng):
    def make():
        d = plain(rng)
        d["w"] = channel(d["w"], alone=True)
        live = np.stack([rng.permutation(np.repeat([0, 1, 2], [T - 2 * (T // 8), T // 8, T // 8])) for r in range(N)])
        for k, e in (("x", live), ("qx", rng.choice(3, (N, G), p=[0.75, 0.125, 0.125]))):
            m = np.repeat(e, 4, axis=1)[:, None, :]
            c = np.where(m == 0, d[k].astype(np.float32), np.float32(0))
            c[:, :8] = np.where(m == 2, np.float32(-4), c[:, :8])
            d[k] = c.astype(BF)
        for r in rng.permutation(N)[:N // 2]: d["u"][r] = signed(d["u"][r], 1, -1)
        return d
    return first(make)
def setup_inputs_spread(rng):
    return first(lambda: {**plain(rng), "x": wide(rng, N, 128, 4 * T, cols=6), "qx": wide(rng, N, 128, 4 * G, cols=6)})
def check_inputs(d):
    b = []
    for k in ("x", "qx", "w", "u", "v"):
        a = np.abs(d[k].astype(np.float32))
        if not (np.isfinite(a).all() and ((a == 0) | (a >= 2.0 ** -30) & (a <= 2.0 ** 30)).all()): b.append("a value of " + k)
    if (d["u"][:, :, 8:].astype(np.float32) != 0).any(): b.append("u has numbers behind its first two columns")
    if not b and not fit(d): b.append("a number that a layer makes")
    return b
def reference(x, qx, w, u, v):
    log, said, s, num, made = game(x, qx, w, u)
    M = R * CS + T
    oc, osc = np.zeros((N, 128, 4 * M), np.uint8), np.zeros((N, 16, M), np.uint8)
    sid, y = np.full((N, 1, M), -1, np.float32), np.zeros((N, 128, T), np.float32)
    for r in range(N):
        n = len(said[r])
        oc[r], osc[r] = emit(pick(join(*log[r], s[r]), np.concatenate([np.arange(n), np.full(R * CS - n, -1), n + np.arange(T)])))
        sid[r, 0, :n] = said[r]
        sid[r, 0, R * CS:] = num[r]
        y[r] = mx_ref.matmul(mx_ref.quantize(np.ascontiguousarray(v[r])), s[r])
    return {"oc": oc, "osc": osc, "sid": sid, "y": y}

@@ -1,0 +1,642 @@
+from concourse.bass import DstId, RemoteDMATransfer
+from concourse.mybir import dt, AluOpType, AxisListType, ActivationFunctionType
+
+A = AluOpType
+F = ActivationFunctionType
+f8, u8, f32, bf, i32, u16 = "float8_e4m3fn_x4", "uint8", "float32", "bfloat16", "int32", "uint16"
+BIG = 1e29
+NP1, NP3, NPX = 18, 18, 6
+SCRATCH = {}
+for _w, _d, _ns in ((512, bf, "xt qt vt ua ub"), (2048, bf, "wt"), (8, bf, "ut"), (128, bf, "one nul"), (1024, bf, "h0 h1 h2 h3"),
+                    (96, f32, "y_sb"), (224, f32, "sidb"), (128, f32, "nl j16 thr keep sat zero gf"), (1, i32, "pi q16i q8i"),
+                    (1, f32, "q16 q8 hh"), (2, f32, "e1 kb c3"), (16, f32, "w16 cl1 cl2 cl3 cl4"), (8, f32, "c16 pw pwr"),
+                    (8, i32, "pwi pwri i4 i5"), (6, u16, "lgl"), (64, f32, "lz"), (1632, f32, "f1 f2 f3 f4"),
+                    (96, i32, "n1 n2 n3 n4"), (64, u16, "o1 o2 o3 o4"), (256, f32, "num1 num2 num3 num4")):
+    for _n in _ns.split():
+        SCRATCH[_n] = ("sbuf", [128, _w], _d)
+for _w, _ns in ((128, "xq qc uq un vq fin lg land1 land2 land3 ex3 land4"), (512, "wq"), (256, "sr1 sr2 sr3 cat1 cat2 cat3"), (160, "cat4"), (96, "lgo")):
+    for _n in _ns.split():
+        SCRATCH[_n] = ("sbuf", [128, _w], f8)
+        SCRATCH[_n + "_s"] = ("sbuf", [128, _w], u8)
+for _n in ("psA", "psB", "psC", "psD"):
+    SCRATCH[_n] = ("psum", [128, 1024], f32)
+SEMAPHORES = ["ev", "es", "et", "eg", "loc"] + ["m%d" % t for t in range(1, 5)] + ["r%d" % t for t in range(1, 5)] + ["d%d" % i for i in range(40)]
+
+
+def fan(topo, src, dsts):
+    off = [i for i, d in enumerate(dsts) if topo.chip(d) != topo.chip(src)]
+    on = [i for i, d in enumerate(dsts) if topo.chip(d) == topo.chip(src)]
+    out = [None] * len(dsts)
+    used = []
+    for part in (off, on):
+        if not part:
+            continue
+        pool = [e for e in topo.engines(src, dsts[part[0]]) if e not in used]
+        if part is on and not used:
+            pool = pool[len(pool) // 2:]
+        k = 1
+        while 2 * k * len(part) <= len(pool):
+            k *= 2
+        for j, i in enumerate(part):
+            out[i] = pool[j * k:(j + 1) * k]
+        used += pool
+    return out
+
+
+def rank_program(g, core, T, topo):
+    r = T.rank_of(core)
+    if r is None:
+        return
+    C = T.cores
+    N = len(C)
+    others = [q for q in range(N) if q != r]
+    eng = {"v": g.vector, "s": g.scalar, "t": g.tensor, "g": g, "y": g.sync}
+    done = {"v": 0, "s": 0, "t": 0, "g": 0}
+    known = {q: {} for q in eng}
+    snap, hist, waited = {}, {}, {}
+    unit = {}
+    ndma = [0]
+    sent = [0]
+
+    def span(v):
+        n, lo, hi = v[0], v[1], v[2]
+        if n[:2] == "ps":
+            return n, lo // 512 * 512, (hi + 511) // 512 * 512
+        return n, lo, hi
+
+    def deps(q, reads, writes, key):
+        need = {}
+        for isw, vs in ((0, reads), (1, writes)):
+            for v in vs:
+                n, lo, hi = span(v)
+                for (a, b, w, k, i) in hist.get(n, []):
+                    if a >= hi or b <= lo or (k == key == "et" and n[:2] == "ps"):
+                        continue
+                    if not (w or isw or (n[:2] == "ps" and k != key)):
+                        continue
+                    if need.get(k, 0) < i:
+                        need[k] = i
+        for k in sorted(need):
+            i = need[k]
+            if known[q].get(k, 0) >= i:
+                continue
+            eng[q].wait_ge(T.sem[k], i * unit.get(k, 1))
+            waited[k] = max(waited.get(k, 0), i)
+            for kk, ii in snap.get((k, i), {}).items():
+                if known[q].get(kk, 0) < ii:
+                    known[q][kk] = ii
+            known[q][k] = max(known[q].get(k, 0), i)
+
+    def note(reads, writes, key, idx):
+        for isw, vs in ((0, reads), (1, writes)):
+            for v in vs:
+                n, lo, hi = span(v)
+                h = hist.setdefault(n, [])
+                if isw:
+                    h[:] = [e for e in h if not (e[0] >= lo and e[1] <= hi)]
+                else:
+                    h[:] = [e for e in h if not (e[0] >= lo and e[1] <= hi and e[3] == key and not e[2])]
+                h.append((lo, hi, isw, key, idx))
+
+    def op(q, fn, reads, writes):
+        key = "e" + q
+        deps(q, reads, writes, key)
+        done[q] += 1
+        fn(eng[q]).then_inc(T.sem[key], 1)
+        snap[(key, done[q])] = dict(known[q])
+        note(reads, writes, key, done[q])
+
+    def dma(q, out, in_, reads, writes):
+        key = "d%d" % ndma[0]
+        ndma[0] += 1
+        unit[key] = 16
+        deps(q, reads, writes, key)
+        eng[q].dma_start(out, in_).then_inc(T.sem[key], 16)
+        snap[(key, 1)] = dict(known[q])
+        note(reads, writes, key, 1)
+
+    def arrive(key, total, writes):
+        unit[key] = total
+        note([], writes, key, 1)
+
+    def V(n, lo, hi, st=1):
+        return (n, lo, hi, st)
+
+    def ap(v):
+        return T[v[0]][:, v[1]:v[2]] if v[3] == 1 else T[v[0]][:, v[1]:v[2]:v[3]]
+
+    def code(v):
+        return ap(v).bitcast(dt.uint8)
+
+    def pl(v):
+        return (v[0] + "_s",) + v[1:]
+
+    def sc(x):
+        return ap(x) if isinstance(x, tuple) else x
+
+    def rd(*xs):
+        return [x for x in xs if isinstance(x, tuple)]
+
+    def ts(out, in0, s1, op0, s2=None, op1=None):
+        if op1 is None:
+            op("v", lambda e: e.tensor_scalar(ap(out), ap(in0), sc(s1), None, op0), rd(in0, s1), [out])
+        else:
+            op("v", lambda e: e.tensor_scalar(ap(out), ap(in0), sc(s1), sc(s2), op0, op1), rd(in0, s1, s2), [out])
+
+    def tt(out, a, b, o):
+        op("v", lambda e: e.tensor_tensor(ap(out), ap(a), ap(b), o), [a, b], [out])
+
+    def cp(out, a):
+        op("v", lambda e: e.tensor_copy(ap(out), ap(a)), [a], [out])
+
+    def fill(out, c):
+        op("v", lambda e: e.memset(ap(out), c), [], [out])
+
+    def scan(out, d0, d1, init, o0, o1):
+        op("v", lambda e: e.tensor_tensor_scan(ap(out), ap(d0), ap(d1), sc(init), o0, o1), rd(d0, d1, init), [out])
+
+    def red(out, a):
+        op("v", lambda e: e.tensor_reduce(ap(out), ap(a), AxisListType.X, A.add), [a], [out])
+
+    def act(out, a, f, **kw):
+        k2 = {k: sc(x) for k, x in kw.items()}
+        ws = [out] + rd(kw.get("accum_out"))
+        op("s", lambda e: e.activation(ap(out), ap(a), f, **k2), rd(a, kw.get("bias"), kw.get("scale")), ws)
+
+    def quant(out, in_):
+        op("v", lambda e: e.quantize_mx(ap(out), ap(pl(out)), ap(in_)), [in_], [out, pl(out)])
+
+    def mm(out, l, x, start=True, stop=True):
+        op("t", lambda e: e.matmul_mx(ap(out), ap(l), ap(pl(l)), ap(x), ap(pl(x)), start, stop), [l, pl(l), x, pl(x)], [out])
+
+    def pick(out, win, off):
+        op("v", lambda e: e.tensor_copy(ap(out).bitcast(dt.uint32), ap(win).bitcast(dt.uint32).indirect(ap(off))), [win, off], [out])
+        op("s", lambda e: e.activation(ap(pl(out)), ap(pl(win)).indirect(ap(off)), F.Copy), [pl(win), off], [pl(out)])
+
+    def gather(out, win, off):
+        op("s", lambda e: e.activation(ap(out), ap(win).indirect(ap(off)), F.Copy), [win, off], [out])
+
+    def iota(out, pattern, base, cm, isf):
+        if isf:
+            op("g", lambda e: e.iota(ap(out), pattern, base, cm, allow_small_or_imprecise_dtypes=True), [], [out])
+        else:
+            op("g", lambda e: e.iota(ap(out), pattern, base, cm), [], [out])
+
+    def fused(sem, moves):
+        es = fan(topo, core, [C[m[0]] for m in moves])
+        tr, reads = [], []
+        for (d, out, in_, isc), e in zip(moves, es):
+            a = topo.addr(C[d])
+            f = code if isc else ap
+            tr.append(RemoteDMATransfer(dst_ids=[DstId(rid=a[0], pnc=a[1])], dma_engine_mask=sum(1 << k for k in e), remote_sem=T.sem[sem if isinstance(sem, str) else sem[d]], src=f(in_), dst=f(out)))
+            reads.append(in_)
+            sent[0] += len(e)
+        deps("g", reads, [], "remote")
+        g.remote_dma_fused(tr, local_sem=T.sem.loc)
+
+    def plain(sem, mv):
+        fused(sem, mv)
+        fused(sem, [(d, pl(a), pl(b), False) for d, a, b, c in mv])
+
+    def due(calls):
+        n = 0
+        for m in others:
+            for dsts in calls(m):
+                es = fan(topo, C[m], [C[d] for d in dsts])
+                n += sum(len(e) for d, e in zip(dsts, es) if d == r)
+        return n
+
+    def slot(m, d):
+        return (m - d - 1) % N
+
+    def rest(m):
+        return [d for d in range(N) if d != m]
+    ahead = lambda m: [d for d in range(N - 1) if d != m]
+    r1_calls = lambda m: [rest(m), ahead(m)] + ([[N - 1, N - 1]] if m != N - 1 else [])
+    q3_dsts = lambda m: [d for d in (N - 1, 0) if d != m]
+    q4_dsts = lambda m: [d for d in range(1, N) if d != m]
+    np1 = 24 if r == N - 1 else NP1
+    ex = r == N - 1
+    l3 = "ex3" if ex else "land3"
+    l4 = "ex3" if r == 0 else "land4"
+    b4 = 8 * r + (8 if r == 0 else 0)
+    remote = lambda n, b, S, w: [V(n, b + S * s, b + S * s + w) for s in range(N - 1)]
+    both = lambda vs: vs + [pl(v) for v in vs]
+    arrive("r1", due(r1_calls), both(remote("land1", 0, 24, np1)))
+    arrive("r2", due(lambda m: [rest(m)] * 2), both(remote("land2", 8 * r, 32, NPX)))
+    if ex:
+        arrive("r3", due(lambda m: [q3_dsts(m)] * 2), both(remote(l3, 0, 32, NPX)))
+    else:
+        arrive("r3", due(lambda m: [ahead(m)] * 2), both(remote(l3, 0, 32, NP3)))
+    arrive("r4", due(lambda m: [(q3_dsts if r == 0 else q4_dsts)(m)] * 2), both(remote(l4, b4, 32, NPX)))
+    for t in range(1, 5):
+        arrive("m%d" % t, due(lambda m: [rest(m)] if t < 4 or m < N - 1 else []), [V("cl%d" % t, 4 * q, 4 * q + 1) for q in others if t < 4 or q < N - 1])
+
+    dma("y", T.ut[:], T.u[:, 0:8], [], [V("ut", 0, 8)])
+    dma("s", T.qt[:], T.qx[:], [], [V("qt", 0, 512)])
+    dma("y", T.xt[:, 0:384], T.x[:], [], [V("xt", 0, 384)])
+    for i in range(4):
+        c = V("wt", 512 * i, 512 * i + 512)
+        dma("sy"[i % 2], ap(c), T.w[:, 512 * i:512 * i + 512], [], [c])
+    dma("y", T.vt[:], T.v[:], [], [V("vt", 0, 512)])
+
+    iota(V("pi", 0, 1), [[1, 1]], 0, 1, False)
+    iota(V("c16", 0, 8), [[16, 8]], 0, 0, True)
+    iota(V("j16", 0, 128), [[0, 8], [1, 16]], 0, 0, True)
+    iota(V("gf", 0, 128), [[1, 128]], 0, 0, True)
+    iota(V("num1", 0, 96), [[1, 96]], 96 * r, 0, True)
+    q16, q8, hh, e1, w16 = V("q16", 0, 1), V("q8", 0, 1), V("hh", 0, 1), V("e1", 0, 2), V("w16", 0, 16)
+    pw, pwi, pwr = V("pw", 0, 8), V("pwi", 0, 8), V("pwr", 0, 8)
+    fill(V("nul", 0, 128), 0.0)
+    fill(V("one", 0, 128), 1.0)
+    fill(V("xt", 384, 512), 0.0)
+    fill(V("sat", 0, 128), 7.0)
+    fill(V("f1", 0, 1), 31.0)
+    ts(V("q16i", 0, 1), V("pi", 0, 1), 15, A.bitwise_and)
+    cp(q16, V("q16i", 0, 1))
+    ts(pw, V("c16", 0, 8), q16, A.add)
+    ts(pwr, pw, float(N - 1 - r), A.add)
+    cp(pwi, pw)
+    for i in range(4):
+        act(V("ua", i, 512, 4), V("nul", 0, 128), F.Identity, bias=V("ut", i, i + 1))
+        ts(V("ub", i, 512, 4), V("one", 0, 128), V("ut", 4 + i, 5 + i), A.mult, -1.0, A.mult)
+
+    quant(V("qc", 0, 128), V("qt", 0, 512))
+    fused("r1", [(d, V("land1", 24 * slot(r, d), 24 * slot(r, d) + NP1), V("qc", 0, NP1), True) for d in others])
+    fused("r1", [(d, V("land1_s", 24 * slot(r, d), 24 * slot(r, d) + NP1), V("qc_s", 0, NP1), False) for d in ahead(r)])
+    if r != N - 1:
+        k = 24 * slot(r, N - 1)
+        fused("r1", [(N - 1, V("land1_s", k, k + 24), V("qc_s", 0, 24), False), (N - 1, V("land1", k + NP1, k + 24), V("qc", NP1, 24), True)])
+
+    def park(out, in_):
+        dma("y", code(out), code(in_), [in_], [out])
+        dma("y", ap(pl(out)), ap(pl(in_)), [pl(in_)], [pl(out)])
+    park(V("land1", 72, 72 + np1), V("qc", 0, np1))
+
+    def mult(src, ps, h, n, fast):
+        w = src[2] - src[1]
+        for b in range(4):
+            o = 512 * (b % 2)
+            mm(V(ps, o, o + w), V("wq", 128 * b, 128 * b + 128), src)
+            hv, pv = V(h[0], h[1] + b, h[1] + 4 * n, 4), V(ps, o, o + n)
+            if b % 2 and fast:
+                ts(hv, pv, 0.0, A.max, 0.0625, A.mult)
+            else:
+                act(hv, pv, F.Relu, scale=0.0625)
+
+    def layer(src, ps, h, n, out, fast):
+        mult(src, ps, h, n, fast)
+        quant(out, h)
+
+    def diff(o, x):
+        d = V("psD", o, o + x[2] - x[1])
+        mm(d, V("uq", 0, 128), x, True, False)
+        mm(d, V("un", 0, 128), x, False, True)
+        return d
+
+    quant(V("xq", 0, 128), V("xt", 0, 512))
+    quant(V("uq", 0, 128), V("ua", 0, 512))
+    quant(V("un", 0, 128), V("ub", 0, 512))
+    for i in range(4):
+        quant(V("wq", 128 * i, 128 * i + 128), V("wt", 512 * i, 512 * i + 512))
+    s1, s2, s3, s4 = V("sr1", 0, 128), V("sr2", 0, 128), V("sr3", 0, 128), V("cat4", 0, 128)
+    layer(V("xq", 0, 128), "psA", V("h0", 0, 512), 128, s1, True)
+
+    def fv(t, lo, w=1):
+        return V("f%d" % t, lo, lo + w)
+    S_, CUM, NEW, OLD = 1, 776, 912, 1040
+    OLDS, DLT, DV, NE1, G16, TOT, U1, U2, U3, ACC, PF, BB, KTHR, T2 = 1300, 1304, 1308, 1312, 1316, 1336, 1340, 1348, 1356, 1364, 1368, 1372, 1380, 1416
+    own = lambda t: V("cl%d" % t, 4 * r, 4 * r + 1)
+
+    def count(t, d):
+        ts(fv(t, 136, 128), d, 0.0, A.is_gt, -1.0, A.mult)
+        scan(fv(t, S_, 128), fv(t, 136, 128), V("sat", 0, 128), 31.0, A.add, A.max)
+
+    def fold(t, d):
+        tt(fv(t, 264, 128), d, V("thr", 0, 128), A.is_gt)
+        tt(fv(t, 648, 128), fv(t, 0, 128), fv(t, 264, 128), A.mult)
+        scan(fv(t, 520, 128), V("keep", 0, 128), fv(t, 648, 128), 0.0, A.mult, A.add)
+
+    def stay(t):
+        tt(fv(t, 392, 128), fv(t, 1, 128), fv(t, 0, 128), A.is_ge)
+
+    def mlist(t, dv):
+        z = V("f%d" % t, 535, 648, 16)
+        ts(fv(t, U1, 8), z, 7.5, A.is_ge, dv, A.mult)
+        tt(fv(t, U3, 8), fv(t, U1, 8), z, A.subtract)
+        tt(fv(t, U2, 8), fv(t, U3, 8), pw, A.max)
+        cp(V("o%d" % t, 0, 8), fv(t, U2, 8))
+
+    def signs(t):
+        for c in range(2):
+            act(fv(t, 1500, 128), fv(t, S_, 128), F.Sign, scale=1.0, bias=V("kb", c, c + 1), accum_out=fv(t, ACC + c))
+
+    def logpick(t, src):
+        ts(fv(t, PF, 2), fv(t, ACC, 2), 0.5, A.mult, 64.0, A.add)
+        ts(V("o%d" % t, 8, 10), fv(t, PF, 2), 127.0, A.min)
+        pick(V("lg", 32 * t - 32, 32 * t), src, V("o%d" % t, 8, 10))
+        gather(V("nl", 32 * t - 32, 32 * t), V("num%d" % t, 0, 128), V("o%d" % t, 8, 10))
+
+    def oldsum(t):
+        tt(fv(t, NEW, 128), fv(t, OLD, 128), fv(t, 392, 128), A.mult)
+        red(fv(t, OLDS), fv(t, NEW, 128))
+
+    def wants(t, d, o=0):
+        ts(fv(t, OLD + o, d[2] - d[1]), d, 0.0, A.is_gt)
+
+    def window(t):
+        ts(fv(t, NE1, 2), e1, own(t), A.mult)
+        scan(fv(t, CUM + 1, 128), fv(t, OLD + 128, 128), V("zero", 0, 128), 0.0, A.add, A.add)
+
+    def tell(t):
+        fused("m%d" % t, [(d, V("cl%d" % t, 4 * r, 4 * r + 1), own(t), False) for d in others])
+
+    def jump(t):
+        o = V("o%d" % t, 10, 11)
+        if r == 0:
+            cp(o, fv(t, NE1))
+        else:
+            if r == 1:
+                dl = V("cl%d" % t, 0, 1)
+            else:
+                dl = fv(t, DLT)
+                red(dl, V("cl%d" % t, 0, 4 * r, 4))
+            ts(o, fv(t, NE1), dl, A.add)
+        cum = fv(t, CUM, 129)
+        op("v", lambda e: e.tensor_tensor(ap(fv(t, G16, 16)), ap(cum).indirect(ap(o)), ap(w16), A.mult), [cum, o, w16], [fv(t, G16, 16)])
+        red(fv(t, TOT), fv(t, G16, 16))
+        ts(own(t + 1), fv(t, TOT), fv(t, OLDS), A.add, 24.0, A.min)
+        tell(t + 1)
+        if r == 0:
+            return 159.0
+        ts(fv(t, DV), dl, 159.0, A.add)
+        return fv(t, DV)
+
+    def exact(t, d):
+        tt(fv(t, CUM, 32), V(d[0], d[1], d[1] + 32), fv(t, KTHR, 32), A.is_gt)
+        red(fv(t, TOT), fv(t, CUM, 32))
+        ts(own(t + 1), fv(t, TOT), fv(t, OLDS), A.add, 24.0, A.min)
+        tell(t + 1)
+
+    def kthr(t):
+        ts(fv(t, KTHR, 32), V("gf", 0, 32), own(t), A.is_ge, BIG, A.mult)
+
+    def bases(t):
+        scan(fv(t, BB + 1, 4), V("cl%d" % t, 0, 16, 4), V("zero", 0, 4), 0.0 if t == 1 else fv(t - 1, BB + 4), A.add, A.add)
+
+    def carry(t):
+        cp(fv(t, BB), fv(t - 1, BB + 4))
+
+    def runs(t, k, n, first, step):
+        o, z = V("o%d" % t, k, k + n), "n%d" % t
+        cls = V("cl%d" % t, 4 * first, 4 * first + 4 * step * (n - 1) + 1, 4 * step)
+        bs = V("f%d" % t, BB + first, BB + first + step * (n - 1) + 1, step)
+        ts(fv(t, T2, n), cls, hh, A.mult, float(N - 1 - r), A.add)
+        tt(V(z, 16, 16 + n), fv(t, T2, n), bs, A.add)
+        ts(V(z, 20, 20 + n), V(z, 16, 16 + n), 2, A.arith_shift_right)
+        ts(o, V(z, 20, 20 + n), q8, A.add)
+        return o
+
+    def order(t, B, nc, ib):
+        z = "n%d" % t
+        ts(V(z, 32, 32 + nc), V("pwr", 0, nc), B, A.add, 32.0, A.mult)
+        ts(V(z, 40, 40 + nc), V(z, 32, 32 + nc), 96, A.bitwise_and)
+        tt(V(z, 48, 48 + nc), V(z, 40, 40 + nc), V(ib[0], ib[1], ib[1] + nc), A.add)
+        cp(V("o%d" % t, 24, 24 + nc), V(z, 48, 48 + nc))
+        return V("o%d" % t, 24, 24 + nc)
+
+    def numbers(t, B):
+        if B is None:
+            ts(V("num%d" % t, 128, 256), V("gf", 0, 128), 384.0, A.add)
+        else:
+            ts(V("num%d" % t, 128, 256), V("gf", 0, 128), B, A.add, 384.0, A.add)
+
+    def renumber(t):
+        gather(V("num%d" % (t + 1), 0, 128), V("num%d" % t, 0, 256), V("o%d" % t, 0, 8))
+
+    def log1():
+        ts(V("kb", 0, 2), V("pw", 0, 2), -30.5, A.add)
+        fill(V("num1", 96, 128), -1.0)
+        signs(1)
+        numbers(1, None)
+        logpick(1, s1)
+        renumber(1)
+
+    def log23():
+        signs(2)
+        signs(3)
+        numbers(2, fv(2, BB + r))
+        numbers(3, fv(3, BB + 3) if ex else fv(2, BB + 4))
+        logpick(2, s2)
+        renumber(2)
+        logpick(3, s3)
+        renumber(3)
+
+    lz = lambda a, w=1: V("lz", a, a + w)
+
+    def gaps():
+        scan(lz(1), own(1), V("zero", 0, 1), 0.0, A.add, A.add)
+        scan(lz(2), own(2), V("zero", 0, 1), lz(1), A.add, A.add)
+        for t in range(1, 4):
+            ts(lz(8 + t), own(t), -1.0, A.mult, 32.0, A.add)
+        scan(lz(3), own(3), V("zero", 0, 1), lz(2), A.add, A.add)
+        for t in range(1, 4):
+            ts(lz(12 + 6 * t, 6), V("pw", 0, 6), lz(t), A.is_ge, lz(8 + t), A.mult)
+        tt(lz(12, 6), lz(18, 6), lz(24, 6), A.add)
+        tt(lz(36, 6), lz(30, 6), V("pw", 0, 6), A.add)
+        tt(lz(42, 6), lz(12, 6), lz(36, 6), A.add)
+        ts(V("lgl", 0, 6), lz(42, 6), 127.0, A.min)
+
+    d1 = diff(0, s1)
+    count(1, d1)
+    ts(own(1), fv(1, 128), -1.0, A.mult, 31.0, A.add)
+    tell(1)
+    mult(s1, "psA", V("h1", 0, 512), 128, True)
+    stay(1)
+    cp(V("pwri", 0, 8), pwr)
+    ts(V("i4", 0, 8), pwi, 2, A.arith_shift_right)
+    ts(V("n1", 56, 64), V("pwri", 0, 8), 3, A.bitwise_and)
+    ts(V("n1", 72, 80), V("i4", 0, 8), float(np1 - 1), A.min)
+    ts(V("n1", 64, 72), V("n1", 56, 64), 24.0, A.mult)
+    quant(V("cat1", 0, 128), V("h1", 0, 512))
+    p1 = diff(512, V("cat1", 0, 128))
+    tt(V("n1", 80, 88), V("n1", 64, 72), V("n1", 72, 80), A.add)
+    cp(V("o1", 24, 32), V("n1", 80, 88))
+    fill(V("zero", 0, 128), 0.0)
+    fill(w16, 0.0)
+    fill(e1, 0.0)
+    fill(fv(1, CUM), 0.0)
+    ts(V("thr", 0, 128), V("j16", 0, 128), q16, A.not_equal, BIG, A.mult)
+    fill(V("w16", 0, 1), -1.0)
+    fill(V("w16", 1, 2), 1.0)
+    ts(V("e1", 0, 1), q16, 1.0, A.is_equal)
+    ts(V("keep", 0, 128), V("j16", 0, 128), 0.5, A.is_gt)
+    wants(1, p1)
+    oldsum(1)
+    pick(V("sr1", 128, 256), V("land1", 0, 96), V("o1", 24, 32))
+    layer(V("sr1", 128, 256), "psA", V("h1", 512, 1024), 128, V("cat1", 128, 256), True)
+    wants(1, diff(512, V("cat1", 128, 256)), 128)
+    window(1)
+    m1d = jump(1)
+    fold(1, d1)
+    mlist(1, m1d)
+    pick(s2, V("cat1", 0, 256), V("o1", 0, 8))
+    d2 = diff(0, s2)
+    mult(s2, "psB", V("h2", 0, 512), 128, False)
+    bases(1)
+    carry(2)
+    ts(V("q8i", 0, 1), V("pi", 0, 1), 7, A.bitwise_and)
+    ts(hh, q16, 7.5, A.is_gt)
+    cp(q8, V("q8i", 0, 1))
+    fill(V("c3", 0, 2), float(N - 1 - r))
+    fill(V("f2", 0, 1), 31.0)
+    park(V("sr2", 160, 256), V("qc", 0, 96))
+    if ex:
+        park(V("sr3", 160, 256), V("qc", 0, 96))
+    count(2, d2)
+    log1()
+    bases(2)
+    o = runs(2, 16, 2, 0, 2)
+    pick(V("land2", 96, 128), V("qc", 0, 128), o)
+    land = lambda n, b, d: V(n, b + 32 * slot(r, d), b + 32 * slot(r, d) + NPX)
+    plain("r2", [(d, land("land2", 8 * d, d), V("land2", 96 + 8 * d, 96 + 8 * d + NPX), True) for d in others])
+    z = "n3"
+    ts(V(z, 56, 58), V("c3", 0, 2), fv(2, BB + 4), A.add)
+    ts(V(z, 58, 60), V(z, 56, 58), 2, A.arith_shift_right)
+    tt(V(z, 60, 62), V(z, 58, 60), V("pwi", 0, 2), A.add)
+    cp(V("o3", 16, 18), V(z, 60, 62))
+    pick(V("land3", 96, 128), V("qc", 0, 128), V("o3", 16, 18))
+    plain("r3", [(d, V("land3", 32 * slot(r, d), 32 * slot(r, d) + NP3), V("land3", 96, 96 + NP3), True) for d in ahead(r)])
+    quant(V("cat2", 0, 128), V("h2", 0, 512))
+    p2 = diff(512, V("cat2", 0, 128))
+    stay(2)
+    kthr(2)
+    ts(V("i5", 0, 8), V("i4", 0, 8), float(NPX - 1), A.min)
+    fill(V("h2", 640, 1024), 0.0)
+    ts(V("n2", 56, 64), V("i5", 0, 8), float(8 * r), A.add)
+    wants(2, p2)
+    gl2 = order(2, fv(2, BB + r), 2, ("n2", 56))
+    oldsum(2)
+    fold(2, d2)
+    mlist(2, 159.0)
+    if not ex:
+        ts(V("n3", 64, 72), V("i4", 0, 8), float(NP3 - 1), A.min)
+        gl3 = order(3, fv(2, BB + 4), 8, ("n3", 64))
+    pick(V("sr2", 128, 160), V("land2", 0, 128), gl2)
+    layer(V("sr2", 128, 256), "psB", V("h2", 512, 1024), 32, V("cat2", 128, 256), True)
+    w2 = diff(512, V("cat2", 128, 256))
+    fill(V("f3", 0, 1), 31.0)
+    fill(V("f4", 0, 1), 31.0)
+    fill(fv(3, CUM), 0.0)
+    fill(V("cl4", 12, 16), 0.0)
+    if not ex:
+        pick(V("sr3", 128, 256), V("land3", 0, 128), gl3)
+        mult(V("sr3", 128, 256), "psC", V("h3", 512, 1024), 128, False)
+    exact(2, w2)
+    pick(s3, V("cat2", 0, 256), V("o2", 0, 8))
+    if not ex:
+        quant(V("cat3", 128, 256), V("h3", 512, 1024))
+        w3 = diff(512, V("cat3", 128, 256))
+        mult(s3, "psC", V("h3", 0, 512), 128, True)
+        d3 = diff(0, s3)
+        carry(3)
+        wants(3, w3, 128)
+        window(3)
+        quant(V("cat3", 0, 128), V("h3", 0, 512))
+        p3 = diff(512, V("cat3", 0, 128))
+        count(3, d3)
+        stay(3)
+        wants(3, p3)
+        oldsum(3)
+        m3d = jump(3)
+    else:
+        mult(s3, "psC", V("h3", 0, 512), 128, False)
+        fill(V("h3", 640, 1024), 0.0)
+        d3 = diff(0, s3)
+        carry(3)
+        count(3, d3)
+        m3d = 159.0
+    bases(3)
+    o = runs(3, 18, 1, 3, 1)
+    pick(V("ex3", 96, 112), V("qc", 0, 128), o)
+    plain({N - 1: "r3", 0: "r4"}, [(d, land("ex3", 8 if d == 0 else 0, d), V("ex3", 104 if d == 0 else 96, (104 if d == 0 else 96) + NPX), True) for d in q3_dsts(r)])
+    carry(4)
+    fold(3, d3)
+    mlist(3, m3d)
+    if ex:
+        quant(V("cat3", 0, 128), V("h3", 0, 512))
+        gl3 = order(3, fv(3, BB + 3), 2, ("i5", 0))
+        log23()
+        gaps()
+    else:
+        pick(s4, V("cat3", 0, 256), V("o3", 0, 8))
+        d4 = diff(0, s4)
+        count(4, d4)
+    bases(4)
+    o = runs(4, 16, 2, 0, 2)
+    pick(V("land4", 96, 128), V("qc", 0, 128), o)
+    plain("r4", [(d, land("land4", 8 * d, d), V("land4", 96 + 8 * d, 96 + 8 * d + NPX), True) for d in q4_dsts(r)])
+    B4 = fv(3, BB + 4) if r == 0 else fv(4, BB + r)
+    ts(V("n4", 64, 72), V("i5", 0, 8), float(b4), A.add)
+    gl4 = order(4, B4, 2, ("n4", 64))
+    numbers(4, B4)
+    quant(V("vq", 0, 128), V("vt", 0, 512))
+    if ex:
+        pick(V("sr3", 128, 160), V("ex3", 0, 128), gl3)
+        layer(V("sr3", 128, 256), "psC", V("h3", 512, 1024), 32, V("cat3", 128, 256), True)
+        pick(s4, V("cat3", 0, 256), V("o3", 0, 8))
+        d4 = diff(0, s4)
+        count(4, d4)
+        fold(4, d4)
+        mlist(4, 159.0)
+    else:
+        fold(4, d4)
+        mlist(4, 159.0)
+        signs(4)
+        gaps()
+        log23()
+
+    def store(q, colo, src, n):
+        dma(q, T.oc[:, 4 * colo:4 * colo + 4 * n], code(src), [src], [])
+
+    def store_s(qs, colo, src, n):
+        s = pl(src)
+        for k in range(4):
+            dma(qs[k], T.osc[4 * k:4 * k + 4, colo:colo + n], T[s[0]][32 * k:32 * k + 4, s[1]:s[1] + n], [s], [])
+
+    def finish_log():
+        logpick(4, s4)
+        pick(V("lgo", 0, 96), V("lg", 0, 128), V("lgl", 0, 6))
+        gather(V("sidb", 0, 96), V("nl", 0, 128), V("lgl", 0, 6))
+        store("y", 0, V("lgo", 0, 96), 96)
+        store_s("yyyy", 0, V("lgo", 0, 96), 96)
+        dma("y", T.sid[:, 0:96], T.sidb[0:1, 0:96], [V("sidb", 0, 96)], [])
+
+    def finish_places():
+        pick(V("cat4", 128, 160), V(l4, 0, 128), gl4)
+        pick(V("fin", 0, 128), V("cat4", 0, 160), V("o4", 0, 8))
+        mm(V("psD", 512, 640), V("vq", 0, 128), V("fin", 0, 128))
+        store("y", 96, V("fin", 0, 96), 96)
+        store_s("sysy", 96, V("fin", 0, 96), 96)
+        cp(V("y_sb", 0, 96), V("psD", 512, 608))
+        dma("y", T.y[:], T.y_sb[:], [V("y_sb", 0, 96)], [])
+
+    if not ex:
+        finish_log()
+    gather(V("sidb", 96, 224), V("num4", 0, 256), V("o4", 0, 8))
+    if ex:
+        signs(4)
+    dma("y", T.sid[:, 96:192], T.sidb[0:1, 96:192], [V("sidb", 96, 224)], [])
+    finish_places()
+    if ex:
+        finish_log()
+
+    for k in range(ndma[0]):
+        if waited.get("d%d" % k, 0) < 1:
+            g.sync.wait_ge(T.sem["d%d" % k], 16)
+    for q in "vstg":
+        g.wait_ge(T.sem["e" + q], done[q])
+    for t in range(1, 5):
+        g.wait_ge(T.sem["m%d" % t], unit["m%d" % t])
+        g.wait_ge(T.sem["r%d" % t], unit["r%d" % t])
+    g.wait_ge(T.sem.loc, sent[0])

@@ -6,9 +6,11 @@ F = ActivationFunctionType
 f8, u8, f32, bf, i32, u16 = "float8_e4m3fn_x4", "uint8", "float32", "bfloat16", "int32", "uint16"
 BIG = 1e29
 NP1, NP3, NPX = 18, 18, 6
+SEM, MORE, HOP = 0.08, 2.0, {"r1": 4.0, "m1": 2.2, "m2": 2.2, "r2": 2.6, "r3": 3.4, "r3x": 2.6, "m3": 2.2, "m4": 2.2, "r4": 2.6}
+STAGES = ("r1", "m1", "m2", "r2", "r3", "m3", "m4", "q3", "r4")
 SCRATCH = {}
 for _w, _d, _ns in ((512, bf, "xt qt vt ua ub"), (2048, bf, "wt"), (8, bf, "ut"), (128, bf, "one nul"), (1024, bf, "h0 h1 h2 h3"),
-                    (96, f32, "y_sb"), (224, f32, "sidb"), (128, f32, "nl j16 thr keep sat zero gf"), (1, i32, "pi q16i q8i"),
+                    (96, f32, "y_sb"), (224, f32, "sidb"), (128, f32, "nl j16 thr keep sat zero gf g384"), (1, i32, "pi q16i q8i"),
                     (1, f32, "q16 q8 hh"), (2, f32, "e1 kb c3"), (16, f32, "w16 cl1 cl2 cl3 cl4"), (8, f32, "c16 pw pwr"),
                     (8, i32, "pwi pwri i4 i5"), (6, u16, "lgl"), (64, f32, "lz"), (1632, f32, "f1 f2 f3 f4"),
                     (96, i32, "n1 n2 n3 n4"), (64, u16, "o1 o2 o3 o4"), (256, f32, "num1 num2 num3 num4")):
@@ -50,10 +52,12 @@ def rank_program(g, core, T, topo):
     C = T.cores
     N = len(C)
     others = [q for q in range(N) if q != r]
+    ex = r == N - 1
     eng = {"v": g.vector, "s": g.scalar, "t": g.tensor, "g": g, "y": g.sync}
     done = {"v": 0, "s": 0, "t": 0, "g": 0}
     known = {q: {} for q in eng}
     snap, hist, waited = {}, {}, {}
+    nodes, seen, arrivals, senders = [], {}, {}, {}
     unit = {}
     ndma = [0]
     sent = [0]
@@ -98,26 +102,116 @@ def rank_program(g, core, T, topo):
                     h[:] = [e for e in h if not (e[0] >= lo and e[1] <= hi and e[3] == key and not e[2])]
                 h.append((lo, hi, isw, key, idx))
 
-    def op(q, fn, reads, writes):
-        key = "e" + q
-        deps(q, reads, writes, key)
-        done[q] += 1
-        fn(eng[q]).then_inc(T.sem[key], 1)
-        snap[(key, done[q])] = dict(known[q])
-        note(reads, writes, key, done[q])
+    def rec(fns, reads, writes, cost, late=0.0):
+        i = len(nodes)
+        pre = set()
+        for isw, vs in ((0, reads), (1, writes)):
+            for v in vs:
+                n, lo, hi = span(v)
+                for (a, b, w, j) in seen.get(n, []):
+                    if a < hi and b > lo and (w or isw or n[:2] == "ps"):
+                        pre.add(j)
+        for isw, vs in ((0, reads), (1, writes)):
+            for v in vs:
+                n, lo, hi = span(v)
+                h = seen.setdefault(n, [])
+                if isw:
+                    h[:] = [e for e in h if not (e[0] >= lo and e[1] <= hi)]
+                h.append((lo, hi, isw, i))
+        nodes.append((fns, reads, writes, cost, late, pre))
+        return i
 
-    def dma(q, out, in_, reads, writes):
-        key = "d%d" % ndma[0]
-        ndma[0] += 1
-        unit[key] = 16
-        deps(q, reads, writes, key)
-        eng[q].dma_start(out, in_).then_inc(T.sem[key], 16)
-        snap[(key, 1)] = dict(known[q])
-        note(reads, writes, key, 1)
+    def schedule():
+        for key, i in arrivals.items():
+            last = {"m4": "q3", "r3": "q3" if ex else "r3", "r4": "q3" if r == 0 else "r4"}.get(key, key)
+            for st in STAGES[:STAGES.index(last) + 1]:
+                nodes[i][5].update(senders.get(st, []))
+        n = len(nodes)
+        nxt = [[] for _ in range(n)]
+        left = [len(x[5]) for x in nodes]
+        for i, x in enumerate(nodes):
+            for p in x[5]:
+                nxt[p].append(i)
+        order, todo, lf = [], [i for i in range(n) if left[i] == 0], list(left)
+        while todo:
+            i = todo.pop()
+            order.append(i)
+            for j in nxt[i]:
+                lf[j] -= 1
+                if lf[j] == 0:
+                    todo.append(j)
+        rank = [0.0] * n
+        for i in reversed(order):
+            rank[i] = nodes[i][3] + nodes[i][4] + SEM + max([rank[j] for j in nxt[i]] + [0.0])
+        ready = [0.0] * n
+        free = {q: 0.0 for q in eng}
+        avail = [i for i in range(n) if left[i] == 0]
+
+        def finish(i, t):
+            for j in nxt[i]:
+                ready[j] = max(ready[j], t)
+                left[j] -= 1
+                if left[j] == 0:
+                    avail.append(j)
+        while avail:
+            best = None
+            for i in avail:
+                if not nodes[i][0]:
+                    best = (0.0, i, None)
+                    break
+                for q in nodes[i][0]:
+                    s = max(free[q], ready[i])
+                    if best is None or s < best[0]:
+                        best = (s, i, q)
+            q = best[2]
+            if q is None:
+                i = best[1]
+                avail.remove(i)
+                finish(i, ready[i] + nodes[i][4])
+                continue
+            cand = [i for i in avail if q in nodes[i][0] and max(free[q], ready[i]) <= best[0]]
+            i = max(cand, key=lambda i: (rank[i], -i))
+            end = max(free[q], ready[i]) + nodes[i][3]
+            soon = [j for j in avail if q in nodes[j][0] and ready[j] < end - 0.02 and rank[j] > rank[i] + MORE]
+            if soon:
+                i = max(soon, key=lambda i: (rank[i], -i))
+            avail.remove(i)
+            free[q] = max(free[q], ready[i]) + nodes[i][3]
+            issue(q, i)
+            finish(i, free[q] + nodes[i][4] + SEM)
+
+    def issue(q, i):
+        fns, reads, writes = nodes[i][:3]
+        kind, fn = fns[q]
+        if kind == "op":
+            key = "e" + q
+            deps(q, reads, writes, key)
+            done[q] += 1
+            fn(eng[q]).then_inc(T.sem[key], 1)
+            snap[(key, done[q])] = dict(known[q])
+            note(reads, writes, key, done[q])
+        elif kind == "dma":
+            key = "d%d" % ndma[0]
+            ndma[0] += 1
+            unit[key] = 16
+            deps(q, reads, writes, key)
+            fn(eng[q]).then_inc(T.sem[key], 16)
+            snap[(key, 1)] = dict(known[q])
+            note(reads, writes, key, 1)
+        else:
+            deps(q, reads, [], "remote")
+            fn(eng[q])
+
+    def op(q, fn, reads, writes, cost):
+        rec({q: ("op", fn)}, reads, writes, cost)
+
+    def dma(q, out, in_, reads, writes, kib=64):
+        rec({q: ("dma", lambda e: e.dma_start(out, in_))}, reads, writes, 0.08, 2.0 + kib * 0.006)
 
     def arrive(key, total, writes):
         unit[key] = total
         note([], writes, key, 1)
+        arrivals[key] = rec({}, [], writes, 0.0, HOP["r3x" if key == "r3" and ex else key])
 
     def V(n, lo, hi, st=1):
         return (n, lo, hi, st)
@@ -137,50 +231,58 @@ def rank_program(g, core, T, topo):
     def rd(*xs):
         return [x for x in xs if isinstance(x, tuple)]
 
+    def w(v):
+        return (v[2] - v[1] + v[3] - 1) // v[3]
+
+    def vcost(n):
+        return 0.03 + 0.00105 * max(64, n)
+
     def ts(out, in0, s1, op0, s2=None, op1=None):
         if op1 is None:
-            op("v", lambda e: e.tensor_scalar(ap(out), ap(in0), sc(s1), None, op0), rd(in0, s1), [out])
+            op("v", lambda e: e.tensor_scalar(ap(out), ap(in0), sc(s1), None, op0), rd(in0, s1), [out], vcost(w(out)))
         else:
-            op("v", lambda e: e.tensor_scalar(ap(out), ap(in0), sc(s1), sc(s2), op0, op1), rd(in0, s1, s2), [out])
+            op("v", lambda e: e.tensor_scalar(ap(out), ap(in0), sc(s1), sc(s2), op0, op1), rd(in0, s1, s2), [out], vcost(w(out)))
 
     def tt(out, a, b, o):
-        op("v", lambda e: e.tensor_tensor(ap(out), ap(a), ap(b), o), [a, b], [out])
+        op("v", lambda e: e.tensor_tensor(ap(out), ap(a), ap(b), o), [a, b], [out], vcost(w(out) * (1 if a[0][:2] == "ps" else 2)))
 
     def cp(out, a):
-        op("v", lambda e: e.tensor_copy(ap(out), ap(a)), [a], [out])
+        op("v", lambda e: e.tensor_copy(ap(out), ap(a)), [a], [out], vcost(w(out)))
 
     def fill(out, c):
-        op("v", lambda e: e.memset(ap(out), c), [], [out])
+        op("v", lambda e: e.memset(ap(out), c), [], [out], vcost(w(out)))
 
     def scan(out, d0, d1, init, o0, o1):
-        op("v", lambda e: e.tensor_tensor_scan(ap(out), ap(d0), ap(d1), sc(init), o0, o1), rd(d0, d1, init), [out])
+        op("v", lambda e: e.tensor_tensor_scan(ap(out), ap(d0), ap(d1), sc(init), o0, o1), rd(d0, d1, init), [out], vcost(w(out)))
 
     def red(out, a):
-        op("v", lambda e: e.tensor_reduce(ap(out), ap(a), AxisListType.X, A.add), [a], [out])
+        op("v", lambda e: e.tensor_reduce(ap(out), ap(a), AxisListType.X, A.add), [a], [out], vcost(w(a)))
 
     def act(out, a, f, **kw):
         k2 = {k: sc(x) for k, x in kw.items()}
         ws = [out] + rd(kw.get("accum_out"))
-        op("s", lambda e: e.activation(ap(out), ap(a), f, **k2), rd(a, kw.get("bias"), kw.get("scale")), ws)
+        op("s", lambda e: e.activation(ap(out), ap(a), f, **k2), rd(a, kw.get("bias"), kw.get("scale")), ws, vcost(w(out)) + 0.03)
+
+    def relu(out, a):
+        rec({"v": ("op", lambda e: e.tensor_scalar(ap(out), ap(a), 0.0, 0.0625, A.max, A.mult)),
+             "s": ("op", lambda e: e.activation(ap(out), ap(a), F.Relu, scale=0.0625))}, [a], [out], vcost(w(out)))
 
     def quant(out, in_):
-        op("v", lambda e: e.quantize_mx(ap(out), ap(pl(out)), ap(in_)), [in_], [out, pl(out)])
+        op("v", lambda e: e.quantize_mx(ap(out), ap(pl(out)), ap(in_)), [in_], [out, pl(out)], 0.05 + 0.00028 * w(in_))
 
     def mm(out, l, x, start=True, stop=True):
-        op("t", lambda e: e.matmul_mx(ap(out), ap(l), ap(pl(l)), ap(x), ap(pl(x)), start, stop), [l, pl(l), x, pl(x)], [out])
+        op("t", lambda e: e.matmul_mx(ap(out), ap(l), ap(pl(l)), ap(x), ap(pl(x)), start, stop), [l, pl(l), x, pl(x)], [out], 0.05 + 0.001 * (w(x) + 16))
 
     def pick(out, win, off):
-        op("v", lambda e: e.tensor_copy(ap(out).bitcast(dt.uint32), ap(win).bitcast(dt.uint32).indirect(ap(off))), [win, off], [out])
-        op("s", lambda e: e.activation(ap(pl(out)), ap(pl(win)).indirect(ap(off)), F.Copy), [pl(win), off], [pl(out)])
+        op("v", lambda e: e.tensor_copy(ap(out).bitcast(dt.uint32), ap(win).bitcast(dt.uint32).indirect(ap(off))), [win, off], [out], 0.08 + 0.0016 * w(out))
+        gather(pl(out), pl(win), off)
 
     def gather(out, win, off):
-        op("s", lambda e: e.activation(ap(out), ap(win).indirect(ap(off)), F.Copy), [win, off], [out])
+        op("s", lambda e: e.activation(ap(out), ap(win).indirect(ap(off)), F.Copy), [win, off], [out], 0.09 + 0.0016 * w(out))
 
     def iota(out, pattern, base, cm, isf):
-        if isf:
-            op("g", lambda e: e.iota(ap(out), pattern, base, cm, allow_small_or_imprecise_dtypes=True), [], [out])
-        else:
-            op("g", lambda e: e.iota(ap(out), pattern, base, cm), [], [out])
+        kw = {"allow_small_or_imprecise_dtypes": True} if isf else {}
+        op("g", lambda e: e.iota(ap(out), pattern, base, cm, **kw), [], [out], 0.16 + 0.002 * w(out))
 
     def fused(sem, moves):
         es = fan(topo, core, [C[m[0]] for m in moves])
@@ -191,8 +293,8 @@ def rank_program(g, core, T, topo):
             tr.append(RemoteDMATransfer(dst_ids=[DstId(rid=a[0], pnc=a[1])], dma_engine_mask=sum(1 << k for k in e), remote_sem=T.sem[sem if isinstance(sem, str) else sem[d]], src=f(in_), dst=f(out)))
             reads.append(in_)
             sent[0] += len(e)
-        deps("g", reads, [], "remote")
-        g.remote_dma_fused(tr, local_sem=T.sem.loc)
+        i = rec({"g": ("remote", lambda e: e.remote_dma_fused(tr, local_sem=T.sem.loc))}, reads, [], 0.5)
+        senders.setdefault(sem if isinstance(sem, str) else "q3", []).append(i)
 
     def plain(sem, mv):
         fused(sem, mv)
@@ -215,8 +317,7 @@ def rank_program(g, core, T, topo):
     r1_calls = lambda m: [rest(m), ahead(m)] + ([[N - 1, N - 1]] if m != N - 1 else [])
     q3_dsts = lambda m: [d for d in (N - 1, 0) if d != m]
     q4_dsts = lambda m: [d for d in range(1, N) if d != m]
-    np1 = 24 if r == N - 1 else NP1
-    ex = r == N - 1
+    np1 = 24 if ex else NP1
     l3 = "ex3" if ex else "land3"
     l4 = "ex3" if r == 0 else "land4"
     b4 = 8 * r + (8 if r == 0 else 0)
@@ -233,17 +334,18 @@ def rank_program(g, core, T, topo):
         arrive("m%d" % t, due(lambda m: [rest(m)] if t < 4 or m < N - 1 else []), [V("cl%d" % t, 4 * q, 4 * q + 1) for q in others if t < 4 or q < N - 1])
 
     dma("y", T.ut[:], T.u[:, 0:8], [], [V("ut", 0, 8)])
-    dma("s", T.qt[:], T.qx[:], [], [V("qt", 0, 512)])
-    dma("y", T.xt[:, 0:384], T.x[:], [], [V("xt", 0, 384)])
+    dma("s", T.qt[:], T.qx[:], [], [V("qt", 0, 512)], 128)
+    dma("y", T.xt[:, 0:384], T.x[:], [], [V("xt", 0, 384)], 128)
     for i in range(4):
         c = V("wt", 512 * i, 512 * i + 512)
-        dma("sy"[i % 2], ap(c), T.w[:, 512 * i:512 * i + 512], [], [c])
-    dma("y", T.vt[:], T.v[:], [], [V("vt", 0, 512)])
+        dma("sy"[i % 2], ap(c), T.w[:, 512 * i:512 * i + 512], [], [c], 128 * (i // 2 + 2))
+    dma("y", T.vt[:], T.v[:], [], [V("vt", 0, 512)], 500)
 
     iota(V("pi", 0, 1), [[1, 1]], 0, 1, False)
     iota(V("c16", 0, 8), [[16, 8]], 0, 0, True)
     iota(V("j16", 0, 128), [[0, 8], [1, 16]], 0, 0, True)
     iota(V("gf", 0, 128), [[1, 128]], 0, 0, True)
+    iota(V("g384", 0, 128), [[1, 128]], 384, 0, True)
     iota(V("num1", 0, 96), [[1, 96]], 96 * r, 0, True)
     q16, q8, hh, e1, w16 = V("q16", 0, 1), V("q8", 0, 1), V("hh", 0, 1), V("e1", 0, 2), V("w16", 0, 16)
     pw, pwi, pwr = V("pw", 0, 8), V("pwi", 0, 8), V("pwr", 0, 8)
@@ -264,7 +366,7 @@ def rank_program(g, core, T, topo):
     quant(V("qc", 0, 128), V("qt", 0, 512))
     fused("r1", [(d, V("land1", 24 * slot(r, d), 24 * slot(r, d) + NP1), V("qc", 0, NP1), True) for d in others])
     fused("r1", [(d, V("land1_s", 24 * slot(r, d), 24 * slot(r, d) + NP1), V("qc_s", 0, NP1), False) for d in ahead(r)])
-    if r != N - 1:
+    if not ex:
         k = 24 * slot(r, N - 1)
         fused("r1", [(N - 1, V("land1_s", k, k + 24), V("qc_s", 0, 24), False), (N - 1, V("land1", k + NP1, k + 24), V("qc", NP1, 24), True)])
 
@@ -273,23 +375,18 @@ def rank_program(g, core, T, topo):
         dma("y", ap(pl(out)), ap(pl(in_)), [pl(in_)], [pl(out)])
     park(V("land1", 72, 72 + np1), V("qc", 0, np1))
 
-    def mult(src, ps, h, n, fast):
-        w = src[2] - src[1]
+    def mult(src, ps, h, n):
         for b in range(4):
             o = 512 * (b % 2)
-            mm(V(ps, o, o + w), V("wq", 128 * b, 128 * b + 128), src)
-            hv, pv = V(h[0], h[1] + b, h[1] + 4 * n, 4), V(ps, o, o + n)
-            if b % 2 and fast:
-                ts(hv, pv, 0.0, A.max, 0.0625, A.mult)
-            else:
-                act(hv, pv, F.Relu, scale=0.0625)
+            mm(V(ps, o, o + 128), V("wq", 128 * b, 128 * b + 128), src)
+            relu(V(h[0], h[1] + b, h[1] + 4 * n, 4), V(ps, o, o + n))
 
-    def layer(src, ps, h, n, out, fast):
-        mult(src, ps, h, n, fast)
+    def layer(src, ps, h, n, out):
+        mult(src, ps, h, n)
         quant(out, h)
 
     def diff(o, x):
-        d = V("psD", o, o + x[2] - x[1])
+        d = V("psD", o, o + 128)
         mm(d, V("uq", 0, 128), x, True, False)
         mm(d, V("un", 0, 128), x, False, True)
         return d
@@ -300,12 +397,12 @@ def rank_program(g, core, T, topo):
     for i in range(4):
         quant(V("wq", 128 * i, 128 * i + 128), V("wt", 512 * i, 512 * i + 512))
     s1, s2, s3, s4 = V("sr1", 0, 128), V("sr2", 0, 128), V("sr3", 0, 128), V("cat4", 0, 128)
-    layer(V("xq", 0, 128), "psA", V("h0", 0, 512), 128, s1, True)
+    layer(V("xq", 0, 128), "psA", V("h0", 0, 512), 128, s1)
 
     def fv(t, lo, w=1):
         return V("f%d" % t, lo, lo + w)
     S_, CUM, NEW, OLD = 1, 776, 912, 1040
-    OLDS, DLT, DV, NE1, G16, TOT, U1, U2, U3, ACC, PF, BB, KTHR, T2 = 1300, 1304, 1308, 1312, 1316, 1336, 1340, 1348, 1356, 1364, 1368, 1372, 1380, 1416
+    OLDS, DLT, DV, NE1, G16, TOT, U1, U2, U3, ACC, BB, KTHR, T2 = 1300, 1304, 1308, 1312, 1316, 1336, 1340, 1348, 1356, 1364, 1372, 1380, 1416
     own = lambda t: V("cl%d" % t, 4 * r, 4 * r + 1)
 
     def count(t, d):
@@ -329,11 +426,10 @@ def rank_program(g, core, T, topo):
 
     def signs(t):
         for c in range(2):
-            act(fv(t, 1500, 128), fv(t, S_, 128), F.Sign, scale=1.0, bias=V("kb", c, c + 1), accum_out=fv(t, ACC + c))
+            act(fv(t, 1500, 127), fv(t, S_, 127), F.Sign, scale=1.0, bias=V("kb", c, c + 1), accum_out=fv(t, ACC + c))
 
     def logpick(t, src):
-        ts(fv(t, PF, 2), fv(t, ACC, 2), 0.5, A.mult, 64.0, A.add)
-        ts(V("o%d" % t, 8, 10), fv(t, PF, 2), 127.0, A.min)
+        ts(V("o%d" % t, 8, 10), fv(t, ACC, 2), 0.5, A.mult, 63.5, A.add)
         pick(V("lg", 32 * t - 32, 32 * t), src, V("o%d" % t, 8, 10))
         gather(V("nl", 32 * t - 32, 32 * t), V("num%d" % t, 0, 128), V("o%d" % t, 8, 10))
 
@@ -342,7 +438,7 @@ def rank_program(g, core, T, topo):
         red(fv(t, OLDS), fv(t, NEW, 128))
 
     def wants(t, d, o=0):
-        ts(fv(t, OLD + o, d[2] - d[1]), d, 0.0, A.is_gt)
+        ts(fv(t, OLD + o, 128), d, 0.0, A.is_gt)
 
     def window(t):
         ts(fv(t, NE1, 2), e1, own(t), A.mult)
@@ -363,7 +459,7 @@ def rank_program(g, core, T, topo):
                 red(dl, V("cl%d" % t, 0, 4 * r, 4))
             ts(o, fv(t, NE1), dl, A.add)
         cum = fv(t, CUM, 129)
-        op("v", lambda e: e.tensor_tensor(ap(fv(t, G16, 16)), ap(cum).indirect(ap(o)), ap(w16), A.mult), [cum, o, w16], [fv(t, G16, 16)])
+        op("v", lambda e: e.tensor_tensor(ap(fv(t, G16, 16)), ap(cum).indirect(ap(o)), ap(w16), A.mult), [cum, o, w16], [fv(t, G16, 16)], 0.15)
         red(fv(t, TOT), fv(t, G16, 16))
         ts(own(t + 1), fv(t, TOT), fv(t, OLDS), A.add, 24.0, A.min)
         tell(t + 1)
@@ -385,7 +481,7 @@ def rank_program(g, core, T, topo):
         scan(fv(t, BB + 1, 4), V("cl%d" % t, 0, 16, 4), V("zero", 0, 4), 0.0 if t == 1 else fv(t - 1, BB + 4), A.add, A.add)
 
     def carry(t):
-        cp(fv(t, BB), fv(t - 1, BB + 4))
+        act(fv(t, BB), fv(t - 1, BB + 4), F.Copy)
 
     def runs(t, k, n, first, step):
         o, z = V("o%d" % t, k, k + n), "n%d" % t
@@ -406,10 +502,7 @@ def rank_program(g, core, T, topo):
         return V("o%d" % t, 24, 24 + nc)
 
     def numbers(t, B):
-        if B is None:
-            ts(V("num%d" % t, 128, 256), V("gf", 0, 128), 384.0, A.add)
-        else:
-            ts(V("num%d" % t, 128, 256), V("gf", 0, 128), B, A.add, 384.0, A.add)
+        act(V("num%d" % t, 128, 256), V("g384", 0, 128), F.Identity, **({} if B is None else {"bias": B}))
 
     def renumber(t):
         gather(V("num%d" % (t + 1), 0, 128), V("num%d" % t, 0, 256), V("o%d" % t, 0, 8))
@@ -451,7 +544,7 @@ def rank_program(g, core, T, topo):
     count(1, d1)
     ts(own(1), fv(1, 128), -1.0, A.mult, 31.0, A.add)
     tell(1)
-    mult(s1, "psA", V("h1", 0, 512), 128, True)
+    mult(s1, "psA", V("h1", 0, 512), 128)
     stay(1)
     cp(V("pwri", 0, 8), pwr)
     ts(V("i4", 0, 8), pwi, 2, A.arith_shift_right)
@@ -474,7 +567,7 @@ def rank_program(g, core, T, topo):
     wants(1, p1)
     oldsum(1)
     pick(V("sr1", 128, 256), V("land1", 0, 96), V("o1", 24, 32))
-    layer(V("sr1", 128, 256), "psA", V("h1", 512, 1024), 128, V("cat1", 128, 256), True)
+    layer(V("sr1", 128, 256), "psA", V("h1", 512, 1024), 128, V("cat1", 128, 256))
     wants(1, diff(512, V("cat1", 128, 256)), 128)
     window(1)
     m1d = jump(1)
@@ -482,7 +575,7 @@ def rank_program(g, core, T, topo):
     mlist(1, m1d)
     pick(s2, V("cat1", 0, 256), V("o1", 0, 8))
     d2 = diff(0, s2)
-    mult(s2, "psB", V("h2", 0, 512), 128, False)
+    mult(s2, "psB", V("h2", 0, 512), 128)
     bases(1)
     carry(2)
     ts(V("q8i", 0, 1), V("pi", 0, 1), 7, A.bitwise_and)
@@ -523,7 +616,7 @@ def rank_program(g, core, T, topo):
         ts(V("n3", 64, 72), V("i4", 0, 8), float(NP3 - 1), A.min)
         gl3 = order(3, fv(2, BB + 4), 8, ("n3", 64))
     pick(V("sr2", 128, 160), V("land2", 0, 128), gl2)
-    layer(V("sr2", 128, 256), "psB", V("h2", 512, 1024), 32, V("cat2", 128, 256), True)
+    layer(V("sr2", 128, 256), "psB", V("h2", 512, 1024), 32, V("cat2", 128, 256))
     w2 = diff(512, V("cat2", 128, 256))
     fill(V("f3", 0, 1), 31.0)
     fill(V("f4", 0, 1), 31.0)
@@ -531,13 +624,13 @@ def rank_program(g, core, T, topo):
     fill(V("cl4", 12, 16), 0.0)
     if not ex:
         pick(V("sr3", 128, 256), V("land3", 0, 128), gl3)
-        mult(V("sr3", 128, 256), "psC", V("h3", 512, 1024), 128, False)
+        mult(V("sr3", 128, 256), "psC", V("h3", 512, 1024), 128)
     exact(2, w2)
     pick(s3, V("cat2", 0, 256), V("o2", 0, 8))
     if not ex:
         quant(V("cat3", 128, 256), V("h3", 512, 1024))
         w3 = diff(512, V("cat3", 128, 256))
-        mult(s3, "psC", V("h3", 0, 512), 128, True)
+        mult(s3, "psC", V("h3", 0, 512), 128)
         d3 = diff(0, s3)
         carry(3)
         wants(3, w3, 128)
@@ -550,7 +643,7 @@ def rank_program(g, core, T, topo):
         oldsum(3)
         m3d = jump(3)
     else:
-        mult(s3, "psC", V("h3", 0, 512), 128, False)
+        mult(s3, "psC", V("h3", 0, 512), 128)
         fill(V("h3", 640, 1024), 0.0)
         d3 = diff(0, s3)
         carry(3)
@@ -583,7 +676,7 @@ def rank_program(g, core, T, topo):
     quant(V("vq", 0, 128), V("vt", 0, 512))
     if ex:
         pick(V("sr3", 128, 160), V("ex3", 0, 128), gl3)
-        layer(V("sr3", 128, 256), "psC", V("h3", 512, 1024), 32, V("cat3", 128, 256), True)
+        layer(V("sr3", 128, 256), "psC", V("h3", 512, 1024), 32, V("cat3", 128, 256))
         pick(s4, V("cat3", 0, 256), V("o3", 0, 8))
         d4 = diff(0, s4)
         count(4, d4)
@@ -630,6 +723,7 @@ def rank_program(g, core, T, topo):
     finish_places()
     if ex:
         finish_log()
+    schedule()
 
     for k in range(ndma[0]):
         if waited.get("d%d" % k, 0) < 1:

from concourse.bass import DstId, RemoteDMATransfer
from concourse.mybir import dt, AluOpType, AxisListType, ActivationFunctionType

A = AluOpType
F = ActivationFunctionType
f8, u8, f32, bf, i32, u16 = "float8_e4m3fn_x4", "uint8", "float32", "bfloat16", "int32", "uint16"
BIG = 1e29
NP1, NP3, NPX = 18, 18, 6
SEM, MORE, HOP = 0.08, 2.0, {"r1": 4.0, "m1": 2.2, "m2": 2.2, "r2": 2.6, "r3": 3.4, "r3x": 2.6, "m3": 2.2, "m4": 2.2, "r4": 2.6}
STAGES = ("r1", "m1", "m2", "r2", "r3", "m3", "m4", "q3", "r4")
SCRATCH = {}
for _w, _d, _ns in ((512, bf, "xt qt vt ua ub"), (2048, bf, "wt"), (8, bf, "ut"), (128, bf, "one nul"), (1024, bf, "h0 h1 h2 h3"),
                    (96, f32, "y_sb"), (224, f32, "sidb"), (128, f32, "nl j16 thr keep sat zero gf g384"), (1, i32, "pi q16i q8i"),
                    (1, f32, "q16 q8 hh"), (2, f32, "e1 kb c3"), (16, f32, "w16 cl1 cl2 cl3 cl4"), (8, f32, "c16 pw pwr"),
                    (8, i32, "pwi pwri i4 i5"), (6, u16, "lgl"), (64, f32, "lz"), (1632, f32, "f1 f2 f3 f4"),
                    (96, i32, "n1 n2 n3 n4"), (64, u16, "o1 o2 o3 o4"), (256, f32, "num1 num2 num3 num4")):
    for _n in _ns.split():
        SCRATCH[_n] = ("sbuf", [128, _w], _d)
for _w, _ns in ((128, "xq qc uq un vq fin lg land1 land2 land3 ex3 land4"), (512, "wq"), (256, "sr1 sr2 sr3 cat1 cat2 cat3"), (160, "cat4"), (96, "lgo")):
    for _n in _ns.split():
        SCRATCH[_n] = ("sbuf", [128, _w], f8)
        SCRATCH[_n + "_s"] = ("sbuf", [128, _w], u8)
for _n in ("psA", "psB", "psC", "psD"):
    SCRATCH[_n] = ("psum", [128, 1024], f32)
SEMAPHORES = ["ev", "es", "et", "eg", "loc"] + ["m%d" % t for t in range(1, 5)] + ["r%d" % t for t in range(1, 5)] + ["d%d" % i for i in range(40)]


def fan(topo, src, dsts):
    off = [i for i, d in enumerate(dsts) if topo.chip(d) != topo.chip(src)]
    on = [i for i, d in enumerate(dsts) if topo.chip(d) == topo.chip(src)]
    out = [None] * len(dsts)
    used = []
    for part in (off, on):
        if not part:
            continue
        pool = [e for e in topo.engines(src, dsts[part[0]]) if e not in used]
        if part is on and not used:
            pool = pool[len(pool) // 2:]
        k = 1
        while 2 * k * len(part) <= len(pool):
            k *= 2
        for j, i in enumerate(part):
            out[i] = pool[j * k:(j + 1) * k]
        used += pool
    return out


def rank_program(g, core, T, topo):
    r = T.rank_of(core)
    if r is None:
        return
    C = T.cores
    N = len(C)
    others = [q for q in range(N) if q != r]
    ex = r == N - 1
    eng = {"v": g.vector, "s": g.scalar, "t": g.tensor, "g": g, "y": g.sync}
    done = {"v": 0, "s": 0, "t": 0, "g": 0}
    known = {q: {} for q in eng}
    snap, hist, waited = {}, {}, {}
    nodes, seen, arrivals, senders = [], {}, {}, {}
    unit = {}
    ndma = [0]
    sent = [0]

    def span(v):
        n, lo, hi = v[0], v[1], v[2]
        if n[:2] == "ps":
            return n, lo // 512 * 512, (hi + 511) // 512 * 512
        return n, lo, hi

    def deps(q, reads, writes, key):
        need = {}
        for isw, vs in ((0, reads), (1, writes)):
            for v in vs:
                n, lo, hi = span(v)
                for (a, b, w, k, i) in hist.get(n, []):
                    if a >= hi or b <= lo or (k == key == "et" and n[:2] == "ps"):
                        continue
                    if not (w or isw or (n[:2] == "ps" and k != key)):
                        continue
                    if need.get(k, 0) < i:
                        need[k] = i
        for k in sorted(need):
            i = need[k]
            if known[q].get(k, 0) >= i:
                continue
            eng[q].wait_ge(T.sem[k], i * unit.get(k, 1))
            waited[k] = max(waited.get(k, 0), i)
            for kk, ii in snap.get((k, i), {}).items():
                if known[q].get(kk, 0) < ii:
                    known[q][kk] = ii
            known[q][k] = max(known[q].get(k, 0), i)

    def note(reads, writes, key, idx):
        for isw, vs in ((0, reads), (1, writes)):
            for v in vs:
                n, lo, hi = span(v)
                h = hist.setdefault(n, [])
                if isw:
                    h[:] = [e for e in h if not (e[0] >= lo and e[1] <= hi)]
                else:
                    h[:] = [e for e in h if not (e[0] >= lo and e[1] <= hi and e[3] == key and not e[2])]
                h.append((lo, hi, isw, key, idx))

    def rec(fns, reads, writes, cost, late=0.0):
        i = len(nodes)
        pre = set()
        for isw, vs in ((0, reads), (1, writes)):
            for v in vs:
                n, lo, hi = span(v)
                for (a, b, w, j) in seen.get(n, []):
                    if a < hi and b > lo and (w or isw or n[:2] == "ps"):
                        pre.add(j)
        for isw, vs in ((0, reads), (1, writes)):
            for v in vs:
                n, lo, hi = span(v)
                h = seen.setdefault(n, [])
                if isw:
                    h[:] = [e for e in h if not (e[0] >= lo and e[1] <= hi)]
                h.append((lo, hi, isw, i))
        nodes.append((fns, reads, writes, cost, late, pre))
        return i

    def schedule():
        for key, i in arrivals.items():
            last = {"m4": "q3", "r3": "q3" if ex else "r3", "r4": "q3" if r == 0 else "r4"}.get(key, key)
            for st in STAGES[:STAGES.index(last) + 1]:
                nodes[i][5].update(senders.get(st, []))
        n = len(nodes)
        nxt = [[] for _ in range(n)]
        left = [len(x[5]) for x in nodes]
        for i, x in enumerate(nodes):
            for p in x[5]:
                nxt[p].append(i)
        order, todo, lf = [], [i for i in range(n) if left[i] == 0], list(left)
        while todo:
            i = todo.pop()
            order.append(i)
            for j in nxt[i]:
                lf[j] -= 1
                if lf[j] == 0:
                    todo.append(j)
        rank = [0.0] * n
        for i in reversed(order):
            rank[i] = nodes[i][3] + nodes[i][4] + SEM + max([rank[j] for j in nxt[i]] + [0.0])
        ready = [0.0] * n
        free = {q: 0.0 for q in eng}
        avail = [i for i in range(n) if left[i] == 0]

        def finish(i, t):
            for j in nxt[i]:
                ready[j] = max(ready[j], t)
                left[j] -= 1
                if left[j] == 0:
                    avail.append(j)
        while avail:
            best = None
            for i in avail:
                if not nodes[i][0]:
                    best = (0.0, i, None)
                    break
                for q in nodes[i][0]:
                    s = max(free[q], ready[i])
                    if best is None or s < best[0]:
                        best = (s, i, q)
            q = best[2]
            if q is None:
                i = best[1]
                avail.remove(i)
                finish(i, ready[i] + nodes[i][4])
                continue
            cand = [i for i in avail if q in nodes[i][0] and max(free[q], ready[i]) <= best[0]]
            i = max(cand, key=lambda i: (rank[i], -i))
            end = max(free[q], ready[i]) + nodes[i][3]
            soon = [j for j in avail if q in nodes[j][0] and ready[j] < end - 0.02 and rank[j] > rank[i] + MORE]
            if soon:
                i = max(soon, key=lambda i: (rank[i], -i))
            avail.remove(i)
            free[q] = max(free[q], ready[i]) + nodes[i][3]
            issue(q, i)
            finish(i, free[q] + nodes[i][4] + SEM)

    def issue(q, i):
        fns, reads, writes = nodes[i][:3]
        kind, fn = fns[q]
        if kind == "op":
            key = "e" + q
            deps(q, reads, writes, key)
            done[q] += 1
            fn(eng[q]).then_inc(T.sem[key], 1)
            snap[(key, done[q])] = dict(known[q])
            note(reads, writes, key, done[q])
        elif kind == "dma":
            key = "d%d" % ndma[0]
            ndma[0] += 1
            unit[key] = 16
            deps(q, reads, writes, key)
            fn(eng[q]).then_inc(T.sem[key], 16)
            snap[(key, 1)] = dict(known[q])
            note(reads, writes, key, 1)
        else:
            deps(q, reads, [], "remote")
            fn(eng[q])

    def op(q, fn, reads, writes, cost):
        rec({q: ("op", fn)}, reads, writes, cost)

    def dma(q, out, in_, reads, writes, kib=64):
        rec({q: ("dma", lambda e: e.dma_start(out, in_))}, reads, writes, 0.08, 2.0 + kib * 0.006)

    def arrive(key, total, writes):
        unit[key] = total
        note([], writes, key, 1)
        arrivals[key] = rec({}, [], writes, 0.0, HOP["r3x" if key == "r3" and ex else key])

    def V(n, lo, hi, st=1):
        return (n, lo, hi, st)

    def ap(v):
        return T[v[0]][:, v[1]:v[2]] if v[3] == 1 else T[v[0]][:, v[1]:v[2]:v[3]]

    def code(v):
        return ap(v).bitcast(dt.uint8)

    def pl(v):
        return (v[0] + "_s",) + v[1:]

    def sc(x):
        return ap(x) if isinstance(x, tuple) else x

    def rd(*xs):
        return [x for x in xs if isinstance(x, tuple)]

    def w(v):
        return (v[2] - v[1] + v[3] - 1) // v[3]

    def vcost(n):
        return 0.03 + 0.00105 * max(64, n)

    def ts(out, in0, s1, op0, s2=None, op1=None):
        if op1 is None:
            op("v", lambda e: e.tensor_scalar(ap(out), ap(in0), sc(s1), None, op0), rd(in0, s1), [out], vcost(w(out)))
        else:
            op("v", lambda e: e.tensor_scalar(ap(out), ap(in0), sc(s1), sc(s2), op0, op1), rd(in0, s1, s2), [out], vcost(w(out)))

    def tt(out, a, b, o):
        op("v", lambda e: e.tensor_tensor(ap(out), ap(a), ap(b), o), [a, b], [out], vcost(w(out) * (1 if a[0][:2] == "ps" else 2)))

    def cp(out, a):
        op("v", lambda e: e.tensor_copy(ap(out), ap(a)), [a], [out], vcost(w(out)))

    def fill(out, c):
        op("v", lambda e: e.memset(ap(out), c), [], [out], vcost(w(out)))

    def scan(out, d0, d1, init, o0, o1):
        op("v", lambda e: e.tensor_tensor_scan(ap(out), ap(d0), ap(d1), sc(init), o0, o1), rd(d0, d1, init), [out], vcost(w(out)))

    def red(out, a):
        op("v", lambda e: e.tensor_reduce(ap(out), ap(a), AxisListType.X, A.add), [a], [out], vcost(w(a)))

    def act(out, a, f, **kw):
        k2 = {k: sc(x) for k, x in kw.items()}
        ws = [out] + rd(kw.get("accum_out"))
        op("s", lambda e: e.activation(ap(out), ap(a), f, **k2), rd(a, kw.get("bias"), kw.get("scale")), ws, vcost(w(out)) + 0.03)

    def relu(out, a):
        rec({"v": ("op", lambda e: e.tensor_scalar(ap(out), ap(a), 0.0, 0.0625, A.max, A.mult)),
             "s": ("op", lambda e: e.activation(ap(out), ap(a), F.Relu, scale=0.0625))}, [a], [out], vcost(w(out)))

    def quant(out, in_):
        op("v", lambda e: e.quantize_mx(ap(out), ap(pl(out)), ap(in_)), [in_], [out, pl(out)], 0.05 + 0.00028 * w(in_))

    def mm(out, l, x, start=True, stop=True):
        op("t", lambda e: e.matmul_mx(ap(out), ap(l), ap(pl(l)), ap(x), ap(pl(x)), start, stop), [l, pl(l), x, pl(x)], [out], 0.05 + 0.001 * (w(x) + 16))

    def pick(out, win, off):
        op("v", lambda e: e.tensor_copy(ap(out).bitcast(dt.uint32), ap(win).bitcast(dt.uint32).indirect(ap(off))), [win, off], [out], 0.08 + 0.0016 * w(out))
        gather(pl(out), pl(win), off)

    def gather(out, win, off):
        op("s", lambda e: e.activation(ap(out), ap(win).indirect(ap(off)), F.Copy), [win, off], [out], 0.09 + 0.0016 * w(out))

    def iota(out, pattern, base, cm, isf):
        kw = {"allow_small_or_imprecise_dtypes": True} if isf else {}
        op("g", lambda e: e.iota(ap(out), pattern, base, cm, **kw), [], [out], 0.16 + 0.002 * w(out))

    def fused(sem, moves):
        es = fan(topo, core, [C[m[0]] for m in moves])
        tr, reads = [], []
        for (d, out, in_, isc), e in zip(moves, es):
            a = topo.addr(C[d])
            f = code if isc else ap
            tr.append(RemoteDMATransfer(dst_ids=[DstId(rid=a[0], pnc=a[1])], dma_engine_mask=sum(1 << k for k in e), remote_sem=T.sem[sem if isinstance(sem, str) else sem[d]], src=f(in_), dst=f(out)))
            reads.append(in_)
            sent[0] += len(e)
        i = rec({"g": ("remote", lambda e: e.remote_dma_fused(tr, local_sem=T.sem.loc))}, reads, [], 0.5)
        senders.setdefault(sem if isinstance(sem, str) else "q3", []).append(i)

    def plain(sem, mv):
        fused(sem, mv)
        fused(sem, [(d, pl(a), pl(b), False) for d, a, b, c in mv])

    def due(calls):
        n = 0
        for m in others:
            for dsts in calls(m):
                es = fan(topo, C[m], [C[d] for d in dsts])
                n += sum(len(e) for d, e in zip(dsts, es) if d == r)
        return n

    def slot(m, d):
        return (m - d - 1) % N

    def rest(m):
        return [d for d in range(N) if d != m]
    ahead = lambda m: [d for d in range(N - 1) if d != m]
    r1_calls = lambda m: [rest(m), ahead(m)] + ([[N - 1, N - 1]] if m != N - 1 else [])
    q3_dsts = lambda m: [d for d in (N - 1, 0) if d != m]
    q4_dsts = lambda m: [d for d in range(1, N) if d != m]
    np1 = 24 if ex else NP1
    l3 = "ex3" if ex else "land3"
    l4 = "ex3" if r == 0 else "land4"
    b4 = 8 * r + (8 if r == 0 else 0)
    remote = lambda n, b, S, w: [V(n, b + S * s, b + S * s + w) for s in range(N - 1)]
    both = lambda vs: vs + [pl(v) for v in vs]
    arrive("r1", due(r1_calls), both(remote("land1", 0, 24, np1)))
    arrive("r2", due(lambda m: [rest(m)] * 2), both(remote("land2", 8 * r, 32, NPX)))
    if ex:
        arrive("r3", due(lambda m: [q3_dsts(m)] * 2), both(remote(l3, 0, 32, NPX)))
    else:
        arrive("r3", due(lambda m: [ahead(m)] * 2), both(remote(l3, 0, 32, NP3)))
    arrive("r4", due(lambda m: [(q3_dsts if r == 0 else q4_dsts)(m)] * 2), both(remote(l4, b4, 32, NPX)))
    for t in range(1, 5):
        arrive("m%d" % t, due(lambda m: [rest(m)] if t < 4 or m < N - 1 else []), [V("cl%d" % t, 4 * q, 4 * q + 1) for q in others if t < 4 or q < N - 1])

    dma("y", T.ut[:], T.u[:, 0:8], [], [V("ut", 0, 8)])
    dma("s", T.qt[:], T.qx[:], [], [V("qt", 0, 512)], 128)
    dma("y", T.xt[:, 0:384], T.x[:], [], [V("xt", 0, 384)], 128)
    for i in range(4):
        c = V("wt", 512 * i, 512 * i + 512)
        dma("sy"[i % 2], ap(c), T.w[:, 512 * i:512 * i + 512], [], [c], 128 * (i // 2 + 2))
    dma("y", T.vt[:], T.v[:], [], [V("vt", 0, 512)], 500)

    iota(V("pi", 0, 1), [[1, 1]], 0, 1, False)
    iota(V("c16", 0, 8), [[16, 8]], 0, 0, True)
    iota(V("j16", 0, 128), [[0, 8], [1, 16]], 0, 0, True)
    iota(V("gf", 0, 128), [[1, 128]], 0, 0, True)
    iota(V("g384", 0, 128), [[1, 128]], 384, 0, True)
    iota(V("num1", 0, 96), [[1, 96]], 96 * r, 0, True)
    q16, q8, hh, e1, w16 = V("q16", 0, 1), V("q8", 0, 1), V("hh", 0, 1), V("e1", 0, 2), V("w16", 0, 16)
    pw, pwi, pwr = V("pw", 0, 8), V("pwi", 0, 8), V("pwr", 0, 8)
    fill(V("nul", 0, 128), 0.0)
    fill(V("one", 0, 128), 1.0)
    fill(V("xt", 384, 512), 0.0)
    fill(V("sat", 0, 128), 7.0)
    fill(V("f1", 0, 1), 31.0)
    ts(V("q16i", 0, 1), V("pi", 0, 1), 15, A.bitwise_and)
    cp(q16, V("q16i", 0, 1))
    ts(pw, V("c16", 0, 8), q16, A.add)
    ts(pwr, pw, float(N - 1 - r), A.add)
    cp(pwi, pw)
    for i in range(4):
        act(V("ua", i, 512, 4), V("nul", 0, 128), F.Identity, bias=V("ut", i, i + 1))
        ts(V("ub", i, 512, 4), V("one", 0, 128), V("ut", 4 + i, 5 + i), A.mult, -1.0, A.mult)

    quant(V("qc", 0, 128), V("qt", 0, 512))
    fused("r1", [(d, V("land1", 24 * slot(r, d), 24 * slot(r, d) + NP1), V("qc", 0, NP1), True) for d in others])
    fused("r1", [(d, V("land1_s", 24 * slot(r, d), 24 * slot(r, d) + NP1), V("qc_s", 0, NP1), False) for d in ahead(r)])
    if not ex:
        k = 24 * slot(r, N - 1)
        fused("r1", [(N - 1, V("land1_s", k, k + 24), V("qc_s", 0, 24), False), (N - 1, V("land1", k + NP1, k + 24), V("qc", NP1, 24), True)])

    def park(out, in_):
        dma("y", code(out), code(in_), [in_], [out])
        dma("y", ap(pl(out)), ap(pl(in_)), [pl(in_)], [pl(out)])
    park(V("land1", 72, 72 + np1), V("qc", 0, np1))

    def mult(src, ps, h, n):
        for b in range(4):
            o = 512 * (b % 2)
            mm(V(ps, o, o + 128), V("wq", 128 * b, 128 * b + 128), src)
            relu(V(h[0], h[1] + b, h[1] + 4 * n, 4), V(ps, o, o + n))

    def layer(src, ps, h, n, out):
        mult(src, ps, h, n)
        quant(out, h)

    def diff(o, x):
        d = V("psD", o, o + 128)
        mm(d, V("uq", 0, 128), x, True, False)
        mm(d, V("un", 0, 128), x, False, True)
        return d

    quant(V("xq", 0, 128), V("xt", 0, 512))
    quant(V("uq", 0, 128), V("ua", 0, 512))
    quant(V("un", 0, 128), V("ub", 0, 512))
    for i in range(4):
        quant(V("wq", 128 * i, 128 * i + 128), V("wt", 512 * i, 512 * i + 512))
    s1, s2, s3, s4 = V("sr1", 0, 128), V("sr2", 0, 128), V("sr3", 0, 128), V("cat4", 0, 128)
    layer(V("xq", 0, 128), "psA", V("h0", 0, 512), 128, s1)

    def fv(t, lo, w=1):
        return V("f%d" % t, lo, lo + w)
    S_, CUM, NEW, OLD = 1, 776, 912, 1040
    OLDS, DLT, DV, NE1, G16, TOT, U1, U2, U3, ACC, BB, KTHR, T2 = 1300, 1304, 1308, 1312, 1316, 1336, 1340, 1348, 1356, 1364, 1372, 1380, 1416
    own = lambda t: V("cl%d" % t, 4 * r, 4 * r + 1)

    def count(t, d):
        ts(fv(t, 136, 128), d, 0.0, A.is_gt, -1.0, A.mult)
        scan(fv(t, S_, 128), fv(t, 136, 128), V("sat", 0, 128), 31.0, A.add, A.max)

    def fold(t, d):
        tt(fv(t, 264, 128), d, V("thr", 0, 128), A.is_gt)
        tt(fv(t, 648, 128), fv(t, 0, 128), fv(t, 264, 128), A.mult)
        scan(fv(t, 520, 128), V("keep", 0, 128), fv(t, 648, 128), 0.0, A.mult, A.add)

    def stay(t):
        tt(fv(t, 392, 128), fv(t, 1, 128), fv(t, 0, 128), A.is_ge)

    def mlist(t, dv):
        z = V("f%d" % t, 535, 648, 16)
        ts(fv(t, U1, 8), z, 7.5, A.is_ge, dv, A.mult)
        tt(fv(t, U3, 8), fv(t, U1, 8), z, A.subtract)
        tt(fv(t, U2, 8), fv(t, U3, 8), pw, A.max)
        cp(V("o%d" % t, 0, 8), fv(t, U2, 8))

    def signs(t):
        for c in range(2):
            act(fv(t, 1500, 127), fv(t, S_, 127), F.Sign, scale=1.0, bias=V("kb", c, c + 1), accum_out=fv(t, ACC + c))

    def logpick(t, src):
        ts(V("o%d" % t, 8, 10), fv(t, ACC, 2), 0.5, A.mult, 63.5, A.add)
        pick(V("lg", 32 * t - 32, 32 * t), src, V("o%d" % t, 8, 10))
        gather(V("nl", 32 * t - 32, 32 * t), V("num%d" % t, 0, 128), V("o%d" % t, 8, 10))

    def oldsum(t):
        tt(fv(t, NEW, 128), fv(t, OLD, 128), fv(t, 392, 128), A.mult)
        red(fv(t, OLDS), fv(t, NEW, 128))

    def wants(t, d, o=0):
        ts(fv(t, OLD + o, 128), d, 0.0, A.is_gt)

    def window(t):
        ts(fv(t, NE1, 2), e1, own(t), A.mult)
        scan(fv(t, CUM + 1, 128), fv(t, OLD + 128, 128), V("zero", 0, 128), 0.0, A.add, A.add)

    def tell(t):
        fused("m%d" % t, [(d, V("cl%d" % t, 4 * r, 4 * r + 1), own(t), False) for d in others])

    def jump(t):
        o = V("o%d" % t, 10, 11)
        if r == 0:
            cp(o, fv(t, NE1))
        else:
            if r == 1:
                dl = V("cl%d" % t, 0, 1)
            else:
                dl = fv(t, DLT)
                red(dl, V("cl%d" % t, 0, 4 * r, 4))
            ts(o, fv(t, NE1), dl, A.add)
        cum = fv(t, CUM, 129)
        op("v", lambda e: e.tensor_tensor(ap(fv(t, G16, 16)), ap(cum).indirect(ap(o)), ap(w16), A.mult), [cum, o, w16], [fv(t, G16, 16)], 0.15)
        red(fv(t, TOT), fv(t, G16, 16))
        ts(own(t + 1), fv(t, TOT), fv(t, OLDS), A.add, 24.0, A.min)
        tell(t + 1)
        if r == 0:
            return 159.0
        ts(fv(t, DV), dl, 159.0, A.add)
        return fv(t, DV)

    def exact(t, d):
        tt(fv(t, CUM, 32), V(d[0], d[1], d[1] + 32), fv(t, KTHR, 32), A.is_gt)
        red(fv(t, TOT), fv(t, CUM, 32))
        ts(own(t + 1), fv(t, TOT), fv(t, OLDS), A.add, 24.0, A.min)
        tell(t + 1)

    def kthr(t):
        ts(fv(t, KTHR, 32), V("gf", 0, 32), own(t), A.is_ge, BIG, A.mult)

    def bases(t):
        scan(fv(t, BB + 1, 4), V("cl%d" % t, 0, 16, 4), V("zero", 0, 4), 0.0 if t == 1 else fv(t - 1, BB + 4), A.add, A.add)

    def carry(t):
        act(fv(t, BB), fv(t - 1, BB + 4), F.Copy)

    def runs(t, k, n, first, step):
        o, z = V("o%d" % t, k, k + n), "n%d" % t
        cls = V("cl%d" % t, 4 * first, 4 * first + 4 * step * (n - 1) + 1, 4 * step)
        bs = V("f%d" % t, BB + first, BB + first + step * (n - 1) + 1, step)
        ts(fv(t, T2, n), cls, hh, A.mult, float(N - 1 - r), A.add)
        tt(V(z, 16, 16 + n), fv(t, T2, n), bs, A.add)
        ts(V(z, 20, 20 + n), V(z, 16, 16 + n), 2, A.arith_shift_right)
        ts(o, V(z, 20, 20 + n), q8, A.add)
        return o

    def order(t, B, nc, ib):
        z = "n%d" % t
        ts(V(z, 32, 32 + nc), V("pwr", 0, nc), B, A.add, 32.0, A.mult)
        ts(V(z, 40, 40 + nc), V(z, 32, 32 + nc), 96, A.bitwise_and)
        tt(V(z, 48, 48 + nc), V(z, 40, 40 + nc), V(ib[0], ib[1], ib[1] + nc), A.add)
        cp(V("o%d" % t, 24, 24 + nc), V(z, 48, 48 + nc))
        return V("o%d" % t, 24, 24 + nc)

    def numbers(t, B):
        act(V("num%d" % t, 128, 256), V("g384", 0, 128), F.Identity, **({} if B is None else {"bias": B}))

    def renumber(t):
        gather(V("num%d" % (t + 1), 0, 128), V("num%d" % t, 0, 256), V("o%d" % t, 0, 8))

    def log1():
        ts(V("kb", 0, 2), V("pw", 0, 2), -30.5, A.add)
        fill(V("num1", 96, 128), -1.0)
        signs(1)
        numbers(1, None)
        logpick(1, s1)
        renumber(1)

    def log23():
        signs(2)
        signs(3)
        numbers(2, fv(2, BB + r))
        numbers(3, fv(3, BB + 3) if ex else fv(2, BB + 4))
        logpick(2, s2)
        renumber(2)
        logpick(3, s3)
        renumber(3)

    lz = lambda a, w=1: V("lz", a, a + w)

    def gaps():
        scan(lz(1), own(1), V("zero", 0, 1), 0.0, A.add, A.add)
        scan(lz(2), own(2), V("zero", 0, 1), lz(1), A.add, A.add)
        for t in range(1, 4):
            ts(lz(8 + t), own(t), -1.0, A.mult, 32.0, A.add)
        scan(lz(3), own(3), V("zero", 0, 1), lz(2), A.add, A.add)
        for t in range(1, 4):
            ts(lz(12 + 6 * t, 6), V("pw", 0, 6), lz(t), A.is_ge, lz(8 + t), A.mult)
        tt(lz(12, 6), lz(18, 6), lz(24, 6), A.add)
        tt(lz(36, 6), lz(30, 6), V("pw", 0, 6), A.add)
        tt(lz(42, 6), lz(12, 6), lz(36, 6), A.add)
        ts(V("lgl", 0, 6), lz(42, 6), 127.0, A.min)

    d1 = diff(0, s1)
    count(1, d1)
    ts(own(1), fv(1, 128), -1.0, A.mult, 31.0, A.add)
    tell(1)
    mult(s1, "psA", V("h1", 0, 512), 128)
    stay(1)
    cp(V("pwri", 0, 8), pwr)
    ts(V("i4", 0, 8), pwi, 2, A.arith_shift_right)
    ts(V("n1", 56, 64), V("pwri", 0, 8), 3, A.bitwise_and)
    ts(V("n1", 72, 80), V("i4", 0, 8), float(np1 - 1), A.min)
    ts(V("n1", 64, 72), V("n1", 56, 64), 24.0, A.mult)
    quant(V("cat1", 0, 128), V("h1", 0, 512))
    p1 = diff(512, V("cat1", 0, 128))
    tt(V("n1", 80, 88), V("n1", 64, 72), V("n1", 72, 80), A.add)
    cp(V("o1", 24, 32), V("n1", 80, 88))
    fill(V("zero", 0, 128), 0.0)
    fill(w16, 0.0)
    fill(e1, 0.0)
    fill(fv(1, CUM), 0.0)
    ts(V("thr", 0, 128), V("j16", 0, 128), q16, A.not_equal, BIG, A.mult)
    fill(V("w16", 0, 1), -1.0)
    fill(V("w16", 1, 2), 1.0)
    ts(V("e1", 0, 1), q16, 1.0, A.is_equal)
    ts(V("keep", 0, 128), V("j16", 0, 128), 0.5, A.is_gt)
    wants(1, p1)
    oldsum(1)
    pick(V("sr1", 128, 256), V("land1", 0, 96), V("o1", 24, 32))
    layer(V("sr1", 128, 256), "psA", V("h1", 512, 1024), 128, V("cat1", 128, 256))
    wants(1, diff(512, V("cat1", 128, 256)), 128)
    window(1)
    m1d = jump(1)
    fold(1, d1)
    mlist(1, m1d)
    pick(s2, V("cat1", 0, 256), V("o1", 0, 8))
    d2 = diff(0, s2)
    mult(s2, "psB", V("h2", 0, 512), 128)
    bases(1)
    carry(2)
    ts(V("q8i", 0, 1), V("pi", 0, 1), 7, A.bitwise_and)
    ts(hh, q16, 7.5, A.is_gt)
    cp(q8, V("q8i", 0, 1))
    fill(V("c3", 0, 2), float(N - 1 - r))
    fill(V("f2", 0, 1), 31.0)
    park(V("sr2", 160, 256), V("qc", 0, 96))
    if ex:
        park(V("sr3", 160, 256), V("qc", 0, 96))
    count(2, d2)
    log1()
    bases(2)
    o = runs(2, 16, 2, 0, 2)
    pick(V("land2", 96, 128), V("qc", 0, 128), o)
    land = lambda n, b, d: V(n, b + 32 * slot(r, d), b + 32 * slot(r, d) + NPX)
    plain("r2", [(d, land("land2", 8 * d, d), V("land2", 96 + 8 * d, 96 + 8 * d + NPX), True) for d in others])
    z = "n3"
    ts(V(z, 56, 58), V("c3", 0, 2), fv(2, BB + 4), A.add)
    ts(V(z, 58, 60), V(z, 56, 58), 2, A.arith_shift_right)
    tt(V(z, 60, 62), V(z, 58, 60), V("pwi", 0, 2), A.add)
    cp(V("o3", 16, 18), V(z, 60, 62))
    pick(V("land3", 96, 128), V("qc", 0, 128), V("o3", 16, 18))
    plain("r3", [(d, V("land3", 32 * slot(r, d), 32 * slot(r, d) + NP3), V("land3", 96, 96 + NP3), True) for d in ahead(r)])
    quant(V("cat2", 0, 128), V("h2", 0, 512))
    p2 = diff(512, V("cat2", 0, 128))
    stay(2)
    kthr(2)
    ts(V("i5", 0, 8), V("i4", 0, 8), float(NPX - 1), A.min)
    fill(V("h2", 640, 1024), 0.0)
    ts(V("n2", 56, 64), V("i5", 0, 8), float(8 * r), A.add)
    wants(2, p2)
    gl2 = order(2, fv(2, BB + r), 2, ("n2", 56))
    oldsum(2)
    fold(2, d2)
    mlist(2, 159.0)
    if not ex:
        ts(V("n3", 64, 72), V("i4", 0, 8), float(NP3 - 1), A.min)
        gl3 = order(3, fv(2, BB + 4), 8, ("n3", 64))
    pick(V("sr2", 128, 160), V("land2", 0, 128), gl2)
    layer(V("sr2", 128, 256), "psB", V("h2", 512, 1024), 32, V("cat2", 128, 256))
    w2 = diff(512, V("cat2", 128, 256))
    fill(V("f3", 0, 1), 31.0)
    fill(V("f4", 0, 1), 31.0)
    fill(fv(3, CUM), 0.0)
    fill(V("cl4", 12, 16), 0.0)
    if not ex:
        pick(V("sr3", 128, 256), V("land3", 0, 128), gl3)
        mult(V("sr3", 128, 256), "psC", V("h3", 512, 1024), 128)
    exact(2, w2)
    pick(s3, V("cat2", 0, 256), V("o2", 0, 8))
    if not ex:
        quant(V("cat3", 128, 256), V("h3", 512, 1024))
        w3 = diff(512, V("cat3", 128, 256))
        mult(s3, "psC", V("h3", 0, 512), 128)
        d3 = diff(0, s3)
        carry(3)
        wants(3, w3, 128)
        window(3)
        quant(V("cat3", 0, 128), V("h3", 0, 512))
        p3 = diff(512, V("cat3", 0, 128))
        count(3, d3)
        stay(3)
        wants(3, p3)
        oldsum(3)
        m3d = jump(3)
    else:
        mult(s3, "psC", V("h3", 0, 512), 128)
        fill(V("h3", 640, 1024), 0.0)
        d3 = diff(0, s3)
        carry(3)
        count(3, d3)
        m3d = 159.0
    bases(3)
    o = runs(3, 18, 1, 3, 1)
    pick(V("ex3", 96, 112), V("qc", 0, 128), o)
    plain({N - 1: "r3", 0: "r4"}, [(d, land("ex3", 8 if d == 0 else 0, d), V("ex3", 104 if d == 0 else 96, (104 if d == 0 else 96) + NPX), True) for d in q3_dsts(r)])
    carry(4)
    fold(3, d3)
    mlist(3, m3d)
    if ex:
        quant(V("cat3", 0, 128), V("h3", 0, 512))
        gl3 = order(3, fv(3, BB + 3), 2, ("i5", 0))
        log23()
        gaps()
    else:
        pick(s4, V("cat3", 0, 256), V("o3", 0, 8))
        d4 = diff(0, s4)
        count(4, d4)
    bases(4)
    o = runs(4, 16, 2, 0, 2)
    pick(V("land4", 96, 128), V("qc", 0, 128), o)
    plain("r4", [(d, land("land4", 8 * d, d), V("land4", 96 + 8 * d, 96 + 8 * d + NPX), True) for d in q4_dsts(r)])
    B4 = fv(3, BB + 4) if r == 0 else fv(4, BB + r)
    ts(V("n4", 64, 72), V("i5", 0, 8), float(b4), A.add)
    gl4 = order(4, B4, 2, ("n4", 64))
    numbers(4, B4)
    quant(V("vq", 0, 128), V("vt", 0, 512))
    if ex:
        pick(V("sr3", 128, 160), V("ex3", 0, 128), gl3)
        layer(V("sr3", 128, 256), "psC", V("h3", 512, 1024), 32, V("cat3", 128, 256))
        pick(s4, V("cat3", 0, 256), V("o3", 0, 8))
        d4 = diff(0, s4)
        count(4, d4)
        fold(4, d4)
        mlist(4, 159.0)
    else:
        fold(4, d4)
        mlist(4, 159.0)
        signs(4)
        gaps()
        log23()

    def store(q, colo, src, n):
        dma(q, T.oc[:, 4 * colo:4 * colo + 4 * n], code(src), [src], [])

    def store_s(qs, colo, src, n):
        s = pl(src)
        for k in range(4):
            dma(qs[k], T.osc[4 * k:4 * k + 4, colo:colo + n], T[s[0]][32 * k:32 * k + 4, s[1]:s[1] + n], [s], [])

    def finish_log():
        logpick(4, s4)
        pick(V("lgo", 0, 96), V("lg", 0, 128), V("lgl", 0, 6))
        gather(V("sidb", 0, 96), V("nl", 0, 128), V("lgl", 0, 6))
        store("y", 0, V("lgo", 0, 96), 96)
        store_s("yyyy", 0, V("lgo", 0, 96), 96)
        dma("y", T.sid[:, 0:96], T.sidb[0:1, 0:96], [V("sidb", 0, 96)], [])

    def finish_places():
        pick(V("cat4", 128, 160), V(l4, 0, 128), gl4)
        pick(V("fin", 0, 128), V("cat4", 0, 160), V("o4", 0, 8))
        mm(V("psD", 512, 640), V("vq", 0, 128), V("fin", 0, 128))
        store("y", 96, V("fin", 0, 96), 96)
        store_s("sysy", 96, V("fin", 0, 96), 96)
        cp(V("y_sb", 0, 96), V("psD", 512, 608))
        dma("y", T.y[:], T.y_sb[:], [V("y_sb", 0, 96)], [])

    if not ex:
        finish_log()
    gather(V("sidb", 96, 224), V("num4", 0, 256), V("o4", 0, 8))
    if ex:
        signs(4)
    dma("y", T.sid[:, 96:192], T.sidb[0:1, 96:192], [V("sidb", 96, 224)], [])
    finish_places()
    if ex:
        finish_log()
    schedule()

    for k in range(ndma[0]):
        if waited.get("d%d" % k, 0) < 1:
            g.sync.wait_ge(T.sem["d%d" % k], 16)
    for q in "vstg":
        g.wait_ge(T.sem["e" + q], done[q])
    for t in range(1, 5):
        g.wait_ge(T.sem["m%d" % t], unit["m%d" % t])
        g.wait_ge(T.sem["r%d" % t], unit["r%d" % t])
    g.wait_ge(T.sem.loc, sent[0])
